import numpy as np
import ml_dtypes


def mxq(x, axis, fmt="e4m3"):
    dtype, down = {"e4m3": (ml_dtypes.float8_e4m3fn, 7), "e5m2": (ml_dtypes.float8_e5m2, 14)}[fmt]
    v = np.moveaxis(np.asarray(x, np.float32).astype(ml_dtypes.bfloat16).astype(np.float64), axis, -1)
    blocks = v.reshape(v.shape[:-1] + (-1, 32))
    amax = np.abs(blocks).max(-1, keepdims=True)
    byte = np.maximum(np.where(amax > 0, np.frexp(amax)[1] - 1 + 127, 0) - down, 1)
    scale = np.exp2(byte - 127.0)
    codes = (blocks / scale).astype(np.float32).astype(dtype).astype(np.float64)
    return np.moveaxis((codes * scale).reshape(v.shape), -1, axis)


WIDE = False


def mx_kscale(k):
    if not WIDE:
        return np.ones(k)
    levels = np.array([10, -10, 5, -5, 0])
    if k % 512:
        return np.exp2(np.random.permutation(np.resize(levels, k // 32))).repeat(32)
    a = np.empty((k // 512, 16))
    for p in range(k // 512):
        a[p, :8] = np.random.permutation(np.resize(levels, 8))
        for g in range(8):
            far = levels[np.abs(levels - a[p, g]) >= 10]
            a[p, g + 8] = far[np.random.randint(len(far))]
    return np.exp2(a.ravel()).repeat(32)


def f64(x):
    return np.asarray(x).astype(np.float64)


def striped(idx):
    return np.tile(idx.reshape(-1, 16).T, (8, 1)).astype(np.uint16)


def unstriped(offs):
    return offs[:16].T.reshape(-1).astype(np.int64)


def striped8(idx):
    return np.concatenate([x.reshape(-1, 16).T for x in idx]).astype(np.uint16)


def runs(offs, k):
    lists = np.stack([offs[16 * r : 16 * r + 16].T.reshape(-1) for r in range(8)]).astype(np.int64)
    return lists[np.arange(k) % 512 // 64]


def pack_weight(w):
    k, n = w.shape
    w = f64(np.asarray(w, np.float32).astype(ml_dtypes.bfloat16)).reshape(k // 32, 32, n)
    amax = np.abs(w).max(1)
    byte = np.clip(np.where(amax > 0, np.frexp(amax)[1] - 1 + 127 - 7, 1), 1, 254)
    scaled = (w * np.exp2(127.0 - byte)[:, None, :]).reshape(k, n).astype(np.float32)
    words = np.ascontiguousarray(scaled.reshape(k // 512, 128, 4, n).transpose(0, 1, 3, 2)).astype(ml_dtypes.float8_e4m3fn).view(np.uint8)
    return words, np.ascontiguousarray(byte.astype(np.uint8).reshape(k // 512, 16, n))


def unpack_weight(words, scales):
    g, p, n, _ = words.shape
    vals = np.ascontiguousarray(words).view(ml_dtypes.float8_e4m3fn).astype(np.float64) * np.repeat(np.exp2(scales.astype(np.float64) - 127.0), 8, axis=1)[..., None]
    return vals.transpose(0, 1, 3, 2).reshape(g * 512, n)


def silu(v):
    return v / (1.0 + np.exp(-np.maximum(v, -700.0)))

def planes(y):
    n, m = y.shape
    v = y.astype(np.float32).astype(ml_dtypes.bfloat16).astype(np.float64).reshape(n // 32, 32, m)
    top = np.abs(v).max(1)
    byte = np.clip(np.where(top > 0, np.frexp(top)[1] - 1 + 127 - 7, 1), 1, 254)
    codes = (v * np.exp2(127.0 - byte)[:, None, :]).reshape(n, m).astype(np.float32).astype(ml_dtypes.float8_e4m3fn).view(np.uint8)
    words = codes.reshape(n // 512, 128, 4, m).transpose(0, 1, 3, 2)
    return np.ascontiguousarray(words), np.ascontiguousarray(byte.astype(np.uint8).reshape(n // 512, 16, m))


K, T, S, N, H, U = 1024, 2048, 512, 512, 512, 512


def setup_inputs():
    n = np.random.standard_normal
    s = mx_kscale(K)[:, None]
    u = mx_kscale(H)
    packed_xT = pack_weight(n((K, T)) * s)
    packed_w2 = pack_weight(n((H, N)) / np.sqrt(H) / u[:, None])
    return {
        "x_words": packed_xT[0],
        "x_scales": packed_xT[1],
        "w1": (n((K, H)) / np.sqrt(K) / s * u).astype(np.float32),
        "emb": (0.5 * n((H, U)) * u[:, None]).astype(np.float32),
        "w2_words": packed_w2[0],
        "w2_scales": packed_w2[1],
        "offs": striped(np.random.permutation(T)[:S]),
        "up1": striped8(np.random.randint(0, U, (8, S))),
        "up2": striped8(np.random.randint(0, U, (8, S))),
        "up3": striped8(np.random.randint(0, U, (8, S))),
    }


def reference(x_words, x_scales, w1, emb, w2_words, w2_scales, offs, up1, up2, up3):
    xq = unpack_weight(x_words, x_scales)[:, unstriped(offs)]
    y = mxq(f64(w1), 0, "e4m3").T @ xq
    z = silu(y + f64(emb)[np.arange(H)[:, None], runs(up1, H)] + f64(emb)[np.arange(H)[:, None], runs(up2, H)] + f64(emb)[np.arange(H)[:, None], runs(up3, H)])
    out_0 = unpack_weight(w2_words, w2_scales).T @ mxq(z, 0, "e4m3")
    return (out_0,) + planes(out_0)

@@ -1,0 +1,217 @@
+from contextlib import ExitStack
+
+import concourse.mybir as mybir
+
+K, T, S, N, H, U = 1024, 2048, 512, 512, 512, 512
+FLOPS = 2 * K * H * S + 2 * H * N * S
+
+F32 = mybir.dt.float32
+BF16 = mybir.dt.bfloat16
+I32 = mybir.dt.int32
+U32 = mybir.dt.uint32
+U16 = mybir.dt.uint16
+U8 = mybir.dt.uint8
+FP8X4 = mybir.dt.float8_e4m3fn_x4
+ADD = mybir.AluOpType.add
+SILU = mybir.ActivationFunctionType.Silu
+
+P = 128
+PACK = 4
+PASSES = K // (P * PACK)
+PIECE = 128
+HALF = 256
+QUADS = 4
+
+
+def tile_picked_anc8_silu_po_kernel(
+    tc, x_words, x_scales, w1, emb, w2_words, w2_scales, offs, up1, up2, up3, out_0, out_1, out_2
+):
+    nc = tc.nc
+    with ExitStack() as ctx:
+        sb = ctx.enter_context(tc.tile_pool(name="sb", bufs=1))
+        ps = ctx.enter_context(tc.psum_pool(name="ps", bufs=1))
+
+        def tile(shape, dtype, name):
+            return sb.tile(shape, dtype, name=name, align_bytes=64)
+
+        def entries(lst, a, b):
+            return lst[:, a // 16 : b // 16]
+
+        lists = [tile([P, S // 16], U16, "up%d" % n) for n in range(3)]
+        picked = tile([P, S // 16], U16, "picked")
+        table = [tile([P, U], F32, "table%d" % t) for t in range(PACK)]
+        w1_raw = [[tile([P, PACK, HALF], F32, "w1_raw%d%d" % (g, h)) for h in range(2)] for g in range(PASSES)]
+        x_all = [tile([P, T], I32, "x_all%d" % g) for g in range(PASSES)]
+        xs_all = tile([P, T], U8, "xs_all")
+        w2_raw = tile([P, N], I32, "w2_raw")
+        w2s_raw = tile([P, N], U8, "w2s_raw")
+        warm = tile([P, 1], F32, "warm")
+        warm2 = tile([P, 1], F32, "warm2")
+
+        nc.gpsimd.memset(xs_all[:].bitcast(I32), 0)
+        nc.gpsimd.memset(w2s_raw[:].bitcast(I32), 0)
+        nc.gpsimd.memset(warm[:], 0.0)
+        nc.scalar.activation(warm2[:], warm[:], SILU)
+
+        emb_rows = emb.rearrange("(p t) u -> t p u", t=PACK)
+        nc.sync.dma_start(lists[0][:], up1)
+        nc.sync.dma_start(table[0][:], emb_rows[0])
+        nc.sync.dma_start(table[1][:], emb_rows[1])
+        nc.sync.dma_start(lists[1][:], up2)
+        nc.sync.dma_start(table[2][:], emb_rows[2])
+        nc.sync.dma_start(table[3][:], emb_rows[3])
+        nc.sync.dma_start(lists[2][:], up3)
+        w1_rows = w1.rearrange("(g p j) c -> g p j c", p=P, j=PACK)
+        for g in range(PASSES):
+            for h in range(2):
+                nc.sync.dma_start(w1_raw[g][h][:], w1_rows[g][:, :, h * HALF : (h + 1) * HALF])
+        nc.sync.dma_start(picked[:], offs)
+        for q in range(QUADS):
+            nc.sync.dma_start(
+                xs_all[32 * q : 32 * q + 4 * PASSES, :].bitcast(I32), x_scales[:, 4 * q : 4 * q + 4, :].bitcast(I32)
+            )
+        for g in range(PASSES):
+            nc.sync.dma_start(x_all[g][:], x_words[g].rearrange("p n t -> p (n t)").bitcast(I32))
+        nc.sync.dma_start(w2_raw[:], w2_words[0].rearrange("p n t -> p (n t)").bitcast(I32))
+        for q in range(QUADS):
+            nc.sync.dma_start(
+                w2s_raw[32 * q : 32 * q + 4, :].bitcast(I32), w2_scales[0, 4 * q : 4 * q + 4, :].bitcast(I32)
+            )
+
+        e1 = tile([P, PACK, HALF], F32, "e1")
+        e2 = tile([P, PACK, HALF], F32, "e2")
+        e3 = tile([P, PACK, HALF], F32, "e3")
+        for t in range(PACK):
+            nc.vector.tensor_copy(e1[:, t, :], table[t][:].indirect(entries(lists[0], 0, HALF)))
+        for t in range(PACK):
+            nc.vector.tensor_tensor(e2[:, t, :], table[t][:].indirect(entries(lists[1], 0, HALF)), e1[:, t, :], ADD)
+        for t in range(PACK):
+            nc.vector.tensor_tensor(e3[:, t, :], table[t][:].indirect(entries(lists[2], 0, HALF)), e2[:, t, :], ADD)
+
+        w1_codes, w1_scales = [], []
+        w1_bf = [tile([P, PACK, P, PACK], BF16, "w1_bf%d" % g) for g in range(PASSES)]
+        for g in range(PASSES):
+            for h in range(2):
+                m0 = h * HALF // PACK
+                nc.scalar.copy(
+                    w1_bf[g][:, :, m0 : m0 + HALF // PACK, :].rearrange("p t m j -> p m t j"),
+                    w1_raw[g][h][:].rearrange("p j (m t) -> p m t j", t=PACK),
+                )
+            w1_codes.append(tile([P, H], U32, "w1_codes%d" % g))
+            w1_scales.append(tile([P, H], U8, "w1_scales%d" % g))
+        xs = tile([P, S], U8, "xs")
+        xg = [tile([P, S], U32, "xg%d" % g) for g in range(PASSES)]
+        y = [ps.tile([P, S], F32, name="y%d" % t) for t in range(PACK)]
+        for g in range(PASSES):
+            nc.vector.quantize_mx(
+                w1_codes[g][:].bitcast(FP8X4), w1_scales[g][:], w1_bf[g][:].rearrange("p t m j -> p (t m j)")
+            )
+            if g == 0:
+                nc.vector.tensor_copy(xs[:], xs_all[:].indirect(picked[:]))
+            nc.vector.tensor_copy(xg[g][:], x_all[g][:].bitcast(U32).indirect(picked[:]))
+            for t in range(PACK):
+                cols = slice(t * P, (t + 1) * P)
+                nc.tensor.matmul_mx(
+                    y[t][:],
+                    lhsT=w1_codes[g][:, cols].bitcast(FP8X4),
+                    lhsT_scale=w1_scales[g][:, cols],
+                    rhs=xg[g][:].bitcast(FP8X4),
+                    rhs_scale=xs[4 * g : P, :],
+                    start=(g == 0),
+                    stop=(g == PASSES - 1),
+                )
+
+        w2_codes = tile([P, N], I32, "w2_codes")
+        w2_sc = tile([P, N], U8, "w2_sc")
+        nc.vector.tensor_copy(
+            w2_codes[:].rearrange("p (t m) -> p m t", t=PACK), w2_raw[:].rearrange("p (m t) -> p m t", t=PACK)
+        )
+        nc.vector.tensor_copy(
+            w2_sc[:].rearrange("p (t m) -> p m t", t=PACK), w2s_raw[:].rearrange("p (m t) -> p m t", t=PACK)
+        )
+
+        u_first = tile([P, PACK, HALF], F32, "u_first")
+        y_sb = tile([P, PACK, HALF], F32, "y_sb")
+        f1 = tile([P, PACK, HALF], F32, "f1")
+        f2 = tile([P, PACK, HALF], F32, "f2")
+        u_last = [tile([P, PACK, PIECE], F32, "u_last%d" % c) for c in range(2)]
+        for t in range(PACK):
+            nc.vector.tensor_tensor(u_first[:, t, :], y[t][:, :HALF], e3[:, t, :], ADD)
+            nc.scalar.copy(y_sb[:, t, :], y[t][:, HALF:])
+
+        out_rows = out_0.rearrange("(p t) j -> p t j", t=PACK)
+        out_words = out_1[0].rearrange("p n t -> p (n t)").bitcast(I32)
+        o_scales = tile([P, S], U8, "o_scales")
+        state = {}
+
+        def activate(c, u):
+            z_bf = tile([P, PIECE, PACK], BF16, "z_bf%d" % c)
+            nc.scalar.activation(z_bf[:], u.rearrange("p t n -> p n t"), SILU)
+            state["z", c] = z_bf
+
+        def second_layer(c):
+            z_codes = tile([P, PIECE], U32, "z_codes%d" % c)
+            z_scales = tile([P, PIECE], U8, "z_scales%d" % c)
+            nc.vector.quantize_mx(
+                z_codes[:].bitcast(FP8X4), z_scales[:], state["z", c][:].rearrange("p n t -> p (n t)")
+            )
+            acc = ps.tile([P, PACK, PIECE], F32, name="acc%d" % c)
+            for t in range(PACK):
+                cols = slice(t * P, (t + 1) * P)
+                nc.tensor.matmul_mx(
+                    acc[:, t, :],
+                    lhsT=w2_codes[:, cols].bitcast(FP8X4),
+                    lhsT_scale=w2_sc[:, cols],
+                    rhs=z_codes[:].bitcast(FP8X4),
+                    rhs_scale=z_scales[:],
+                    start=True,
+                    stop=True,
+                )
+            o_f32 = tile([P, PACK, PIECE], F32, "o_f32%d" % c)
+            o_bf = tile([P, PIECE, PACK], BF16, "o_bf%d" % c)
+            if c == 3:
+                nc.vector.tensor_copy(o_bf[:], acc[:].rearrange("p t n -> p n t"))
+                nc.scalar.copy(o_f32[:], acc[:])
+            else:
+                nc.scalar.copy(o_bf[:], acc[:].rearrange("p t n -> p n t"))
+                nc.scalar.copy(o_f32[:], acc[:])
+            nc.sync.dma_start(out_rows[:, :, c * PIECE : (c + 1) * PIECE], o_f32[:])
+            state["o", c] = o_bf
+
+        def hand_on(c):
+            cols = slice(c * PIECE, (c + 1) * PIECE)
+            o_codes = tile([P, PIECE], I32, "o_codes%d" % c)
+            nc.vector.quantize_mx(
+                o_codes[:].bitcast(FP8X4), o_scales[:, cols], state["o", c][:].rearrange("p n t -> p (n t)")
+            )
+            nc.sync.dma_start(out_words[:, cols], o_codes[:])
+
+        activate(0, u_first[:, :, :PIECE])
+        activate(1, u_first[:, :, PIECE:])
+        for t in range(PACK):
+            nc.vector.tensor_tensor(f1[:, t, :], table[t][:].indirect(entries(lists[0], HALF, S)), y_sb[:, t, :], ADD)
+        second_layer(0)
+        second_layer(1)
+        for t in range(PACK):
+            nc.vector.tensor_tensor(f2[:, t, :], table[t][:].indirect(entries(lists[1], HALF, S)), f1[:, t, :], ADD)
+        hand_on(0)
+        hand_on(1)
+        for c in range(2):
+            a = HALF + c * PIECE
+            for t in range(PACK):
+                nc.vector.tensor_tensor(
+                    u_last[c][:, t, :],
+                    table[t][:].indirect(entries(lists[2], a, a + PIECE)),
+                    f2[:, t, c * PIECE : (c + 1) * PIECE],
+                    ADD,
+                )
+            activate(2 + c, u_last[c][:])
+        second_layer(2)
+        second_layer(3)
+        hand_on(2)
+        hand_on(3)
+        for q in range(QUADS):
+            queue = nc.sync if q % 2 else nc.scalar
+            queue.dma_start(
+                out_2[0, 4 * q : 4 * q + 4, :].bitcast(I32), o_scales[32 * q : 32 * q + 4, :].bitcast(I32)
+            )

@@ -21,6 +21,7 @@ PASSES = K // (P * PACK)
 PIECE = 128
 HALF = 256
 QUADS = 4
+EARLY = 2
 
 
 def tile_picked_anc8_silu_po_kernel(
@@ -31,16 +32,16 @@ def tile_picked_anc8_silu_po_kernel(
         sb = ctx.enter_context(tc.tile_pool(name="sb", bufs=1))
         ps = ctx.enter_context(tc.psum_pool(name="ps", bufs=1))
 
-        def tile(shape, dtype, name):
-            return sb.tile(shape, dtype, name=name, align_bytes=64)
+        def tile(shape, dtype, name, tag=None):
+            return sb.tile(shape, dtype, name=name, tag=tag or name, align_bytes=64)
 
         def entries(lst, a, b):
             return lst[:, a // 16 : b // 16]
 
         lists = [tile([P, S // 16], U16, "up%d" % n) for n in range(3)]
         picked = tile([P, S // 16], U16, "picked")
-        table = [tile([P, U], F32, "table%d" % t) for t in range(PACK)]
-        w1_raw = [[tile([P, PACK, HALF], F32, "w1_raw%d%d" % (g, h)) for h in range(2)] for g in range(PASSES)]
+        table = [tile([P, 2 * U if t < EARLY else U], F32, "table%d" % t) for t in range(PACK)]
+        w1_raw = [tile([P, PACK, H], F32, "w1_raw%d" % g) for g in range(PASSES)]
         x_all = [tile([P, T], I32, "x_all%d" % g) for g in range(PASSES)]
         xs_all = tile([P, T], U8, "xs_all")
         w2_raw = tile([P, N], I32, "w2_raw")
@@ -50,53 +51,50 @@ def tile_picked_anc8_silu_po_kernel(
 
         nc.gpsimd.memset(xs_all[:].bitcast(I32), 0)
         nc.gpsimd.memset(w2s_raw[:].bitcast(I32), 0)
-        nc.gpsimd.memset(warm[:], 0.0)
+        nc.vector.memset(warm[:], 0.0)
+        for t in range(EARLY):
+            nc.vector.memset(table[t][:, U:], 0.0)
         nc.scalar.activation(warm2[:], warm[:], SILU)
 
         emb_rows = emb.rearrange("(p t) u -> t p u", t=PACK)
-        nc.sync.dma_start(lists[0][:], up1)
-        nc.sync.dma_start(table[0][:], emb_rows[0])
-        nc.sync.dma_start(table[1][:], emb_rows[1])
-        nc.sync.dma_start(lists[1][:], up2)
-        nc.sync.dma_start(table[2][:], emb_rows[2])
-        nc.sync.dma_start(table[3][:], emb_rows[3])
-        nc.sync.dma_start(lists[2][:], up3)
         w1_rows = w1.rearrange("(g p j) c -> g p j c", p=P, j=PACK)
-        for g in range(PASSES):
-            for h in range(2):
-                nc.sync.dma_start(w1_raw[g][h][:], w1_rows[g][:, :, h * HALF : (h + 1) * HALF])
+        nc.sync.dma_start(lists[0][:], up1)
+        nc.sync.dma_start(table[0][:, :U], emb_rows[0])
+        nc.sync.dma_start(lists[1][:], up2)
+        nc.sync.dma_start(table[1][:, :U], emb_rows[1])
+        nc.sync.dma_start(w1_raw[0][:], w1_rows[0])
+        nc.sync.dma_start(lists[2][:], up3)
         nc.sync.dma_start(picked[:], offs)
         for q in range(QUADS):
             nc.sync.dma_start(
                 xs_all[32 * q : 32 * q + 4 * PASSES, :].bitcast(I32), x_scales[:, 4 * q : 4 * q + 4, :].bitcast(I32)
             )
+        nc.sync.dma_start(w1_raw[1][:], w1_rows[1])
         for g in range(PASSES):
             nc.sync.dma_start(x_all[g][:], x_words[g].rearrange("p n t -> p (n t)").bitcast(I32))
+        nc.sync.dma_start(table[2][:], emb_rows[2])
+        nc.sync.dma_start(table[3][:], emb_rows[3])
         nc.sync.dma_start(w2_raw[:], w2_words[0].rearrange("p n t -> p (n t)").bitcast(I32))
         for q in range(QUADS):
             nc.sync.dma_start(
                 w2s_raw[32 * q : 32 * q + 4, :].bitcast(I32), w2_scales[0, 4 * q : 4 * q + 4, :].bitcast(I32)
             )
 
-        e1 = tile([P, PACK, HALF], F32, "e1")
-        e2 = tile([P, PACK, HALF], F32, "e2")
-        e3 = tile([P, PACK, HALF], F32, "e3")
-        for t in range(PACK):
-            nc.vector.tensor_copy(e1[:, t, :], table[t][:].indirect(entries(lists[0], 0, HALF)))
-        for t in range(PACK):
-            nc.vector.tensor_tensor(e2[:, t, :], table[t][:].indirect(entries(lists[1], 0, HALF)), e1[:, t, :], ADD)
-        for t in range(PACK):
-            nc.vector.tensor_tensor(e3[:, t, :], table[t][:].indirect(entries(lists[2], 0, HALF)), e2[:, t, :], ADD)
+        e1 = tile([P, EARLY, S], F32, "e1")
+        e2 = tile([P, EARLY, S], F32, "e2")
+        e3 = [tile([P, S], F32, "e3_0")]
+        for t in range(EARLY):
+            nc.vector.tensor_copy(e1[:, t, :], table[t][:].indirect(lists[0][:]))
+        for t in range(EARLY):
+            nc.vector.tensor_tensor(e2[:, t, :], table[t][:].indirect(lists[1][:]), e1[:, t, :], ADD)
+        nc.vector.tensor_tensor(e3[0][:], table[0][:].indirect(lists[2][:]), e2[:, 0, :], ADD)
 
         w1_codes, w1_scales = [], []
         w1_bf = [tile([P, PACK, P, PACK], BF16, "w1_bf%d" % g) for g in range(PASSES)]
         for g in range(PASSES):
-            for h in range(2):
-                m0 = h * HALF // PACK
-                nc.scalar.copy(
-                    w1_bf[g][:, :, m0 : m0 + HALF // PACK, :].rearrange("p t m j -> p m t j"),
-                    w1_raw[g][h][:].rearrange("p j (m t) -> p m t j", t=PACK),
-                )
+            nc.scalar.copy(
+                w1_bf[g][:].rearrange("p t m j -> p m j t"), w1_raw[g][:].rearrange("p j (m t) -> p m j t", t=PACK)
+            )
             w1_codes.append(tile([P, H], U32, "w1_codes%d" % g))
             w1_scales.append(tile([P, H], U8, "w1_scales%d" % g))
         xs = tile([P, S], U8, "xs")
@@ -109,7 +107,7 @@ def tile_picked_anc8_silu_po_kernel(
             if g == 0:
                 nc.vector.tensor_copy(xs[:], xs_all[:].indirect(picked[:]))
             nc.vector.tensor_copy(xg[g][:], x_all[g][:].bitcast(U32).indirect(picked[:]))
-            for t in range(PACK):
+            for t in (2, 0, 3, 1):
                 cols = slice(t * P, (t + 1) * P)
                 nc.tensor.matmul_mx(
                     y[t][:],
@@ -121,6 +119,8 @@ def tile_picked_anc8_silu_po_kernel(
                     stop=(g == PASSES - 1),
                 )
 
+        e3.append(tile([P, S], F32, "e3_1", "x_all1"))
+        nc.vector.tensor_tensor(e3[1][:], table[1][:].indirect(lists[2][:]), e2[:, 1, :], ADD)
         w2_codes = tile([P, N], I32, "w2_codes")
         w2_sc = tile([P, N], U8, "w2_sc")
         nc.vector.tensor_copy(
@@ -130,23 +130,21 @@ def tile_picked_anc8_silu_po_kernel(
             w2_sc[:].rearrange("p (t m) -> p m t", t=PACK), w2s_raw[:].rearrange("p (m t) -> p m t", t=PACK)
         )
 
-        u_first = tile([P, PACK, HALF], F32, "u_first")
-        y_sb = tile([P, PACK, HALF], F32, "y_sb")
-        f1 = tile([P, PACK, HALF], F32, "f1")
-        f2 = tile([P, PACK, HALF], F32, "f2")
-        u_last = [tile([P, PACK, PIECE], F32, "u_last%d" % c) for c in range(2)]
-        for t in range(PACK):
-            nc.vector.tensor_tensor(u_first[:, t, :], y[t][:, :HALF], e3[:, t, :], ADD)
-            nc.scalar.copy(y_sb[:, t, :], y[t][:, HALF:])
+        u = [tile([P, PACK, HALF], F32, "u0")]
+        y_sb = tile([P, PACK - EARLY, S], F32, "y_sb")
 
         out_rows = out_0.rearrange("(p t) j -> p t j", t=PACK)
         out_words = out_1[0].rearrange("p n t -> p (n t)").bitcast(I32)
         o_scales = tile([P, S], U8, "o_scales")
         state = {}
 
-        def activate(c, u):
+        def activate(c):
             z_bf = tile([P, PIECE, PACK], BF16, "z_bf%d" % c)
-            nc.scalar.activation(z_bf[:], u.rearrange("p t n -> p n t"), SILU)
+            nc.scalar.activation(
+                z_bf[:].rearrange("p (c i) t -> p c t i", i=4),
+                u[c // 2][:, :, c % 2 * PIECE : (c % 2 + 1) * PIECE].rearrange("p t (c i) -> p c t i", i=4),
+                SILU,
+            )
             state["z", c] = z_bf
 
         def second_layer(c):
@@ -169,9 +167,11 @@ def tile_picked_anc8_silu_po_kernel(
                 )
             o_f32 = tile([P, PACK, PIECE], F32, "o_f32%d" % c)
             o_bf = tile([P, PIECE, PACK], BF16, "o_bf%d" % c)
-            if c == 3:
-                nc.vector.tensor_copy(o_bf[:], acc[:].rearrange("p t n -> p n t"))
+            if c >= 2:
                 nc.scalar.copy(o_f32[:], acc[:])
+                nc.vector.tensor_copy(
+                    o_bf[:].rearrange("p (c i) t -> p c t i", i=4), o_f32[:].rearrange("p t (c i) -> p c t i", i=4)
+                )
             else:
                 nc.scalar.copy(o_bf[:], acc[:].rearrange("p t n -> p n t"))
                 nc.scalar.copy(o_f32[:], acc[:])
@@ -186,27 +186,46 @@ def tile_picked_anc8_silu_po_kernel(
             )
             nc.sync.dma_start(out_words[:, cols], o_codes[:])
 
-        activate(0, u_first[:, :, :PIECE])
-        activate(1, u_first[:, :, PIECE:])
-        for t in range(PACK):
-            nc.vector.tensor_tensor(f1[:, t, :], table[t][:].indirect(entries(lists[0], HALF, S)), y_sb[:, t, :], ADD)
+        def look_up(dst, t, lst, a, b, src):
+            nc.vector.tensor_tensor(dst, table[t][:].indirect(entries(lst, a, b)), src, ADD)
+
+        def early_add(a, b):
+            for t in range(EARLY):
+                nc.vector.tensor_tensor(u[a // HALF][:, t, :], y[t][:, a:b], e3[t][:, a:b], ADD)
+
+        for a in (0, HALF):
+            for t in range(EARLY, PACK):
+                nc.scalar.copy(y_sb[:, t - EARLY, a : a + HALF], y[t][:, a : a + HALF])
+        early_add(0, HALF)
+        f1 = [tile([P, HALF], F32, "f1_%d" % t) for t in range(2)]
+        f2 = [tile([P, HALF], F32, "f2_%d" % t) for t in range(2)]
+        for t in range(2):
+            look_up(f1[t][:], 2 + t, lists[0], 0, HALF, y_sb[:, t, :HALF])
+        for t in range(2):
+            look_up(f2[t][:], 2 + t, lists[1], 0, HALF, f1[t][:])
+        for t in range(2):
+            look_up(u[0][:, 2 + t, :], 2 + t, lists[2], 0, HALF, f2[t][:])
+        activate(0)
+        activate(1)
+        g1_2 = tile([P, HALF], F32, "g1_2", "f2_0")
+        look_up(g1_2[:], 2, lists[0], HALF, S, y_sb[:, 0, HALF:])
+        u.append(tile([P, PACK, HALF], F32, "u1", "f2_1"))
+        early_add(HALF, S)
         second_layer(0)
+        g1_3 = tile([P, HALF], F32, "g1_3", "z_bf0")
+        look_up(g1_3[:], 3, lists[0], HALF, S, y_sb[:, 1, HALF:])
         second_layer(1)
-        for t in range(PACK):
-            nc.vector.tensor_tensor(f2[:, t, :], table[t][:].indirect(entries(lists[1], HALF, S)), f1[:, t, :], ADD)
+        g2 = tile([P, 2, HALF], F32, "g2", "z_bf1")
+        look_up(g2[:, 0, :], 2, lists[1], HALF, S, g1_2[:])
+        look_up(g2[:, 1, :], 3, lists[1], HALF, S, g1_3[:])
+        for c in (2, 3):
+            for t in range(2):
+                a = c * PIECE
+                look_up(u[1][:, 2 + t, a - HALF : a - HALF + PIECE], 2 + t, lists[2], a, a + PIECE, g2[:, t, a - HALF : a - HALF + PIECE])
+            activate(c)
         hand_on(0)
-        hand_on(1)
-        for c in range(2):
-            a = HALF + c * PIECE
-            for t in range(PACK):
-                nc.vector.tensor_tensor(
-                    u_last[c][:, t, :],
-                    table[t][:].indirect(entries(lists[2], a, a + PIECE)),
-                    f2[:, t, c * PIECE : (c + 1) * PIECE],
-                    ADD,
-                )
-            activate(2 + c, u_last[c][:])
         second_layer(2)
+        hand_on(1)
         second_layer(3)
         hand_on(2)
         hand_on(3)

@@ -19,6 +19,7 @@ P = 128
 PACK = 4
 PASSES = K // (P * PACK)
 PIECE = 128
+PIECES = S // PIECE
 HALF = 256
 QUADS = 4
 EARLY = 2
@@ -35,9 +36,6 @@ def tile_picked_anc8_silu_po_kernel(
         def tile(shape, dtype, name, tag=None):
             return sb.tile(shape, dtype, name=name, tag=tag or name, align_bytes=64)
 
-        def entries(lst, a, b):
-            return lst[:, a // 16 : b // 16]
-
         lists = [tile([P, S // 16], U16, "up%d" % n) for n in range(3)]
         picked = tile([P, S // 16], U16, "picked")
         table = [tile([P, 2 * U if t < EARLY else U], F32, "table%d" % t) for t in range(PACK)]
@@ -51,17 +49,17 @@ def tile_picked_anc8_silu_po_kernel(
 
         nc.gpsimd.memset(xs_all[:].bitcast(I32), 0)
         nc.gpsimd.memset(w2s_raw[:].bitcast(I32), 0)
-        nc.vector.memset(warm[:], 0.0)
+        nc.gpsimd.memset(warm[:], 0.0)
         for t in range(EARLY):
             nc.vector.memset(table[t][:, U:], 0.0)
         nc.scalar.activation(warm2[:], warm[:], SILU)
 
         emb_rows = emb.rearrange("(p t) u -> t p u", t=PACK)
         w1_rows = w1.rearrange("(g p j) c -> g p j c", p=P, j=PACK)
-        nc.sync.dma_start(lists[0][:], up1)
         nc.sync.dma_start(table[0][:, :U], emb_rows[0])
-        nc.sync.dma_start(lists[1][:], up2)
+        nc.sync.dma_start(lists[0][:], up1)
         nc.sync.dma_start(table[1][:, :U], emb_rows[1])
+        nc.sync.dma_start(lists[1][:], up2)
         nc.sync.dma_start(w1_raw[0][:], w1_rows[0])
         nc.sync.dma_start(lists[2][:], up3)
         nc.sync.dma_start(picked[:], offs)
@@ -72,9 +70,9 @@ def tile_picked_anc8_silu_po_kernel(
         nc.sync.dma_start(w1_raw[1][:], w1_rows[1])
         for g in range(PASSES):
             nc.sync.dma_start(x_all[g][:], x_words[g].rearrange("p n t -> p (n t)").bitcast(I32))
+        nc.sync.dma_start(w2_raw[:], w2_words[0].rearrange("p n t -> p (n t)").bitcast(I32))
         nc.sync.dma_start(table[2][:], emb_rows[2])
         nc.sync.dma_start(table[3][:], emb_rows[3])
-        nc.sync.dma_start(w2_raw[:], w2_words[0].rearrange("p n t -> p (n t)").bitcast(I32))
         for q in range(QUADS):
             nc.sync.dma_start(
                 w2s_raw[32 * q : 32 * q + 4, :].bitcast(I32), w2_scales[0, 4 * q : 4 * q + 4, :].bitcast(I32)
@@ -99,7 +97,7 @@ def tile_picked_anc8_silu_po_kernel(
             w1_scales.append(tile([P, H], U8, "w1_scales%d" % g))
         xs = tile([P, S], U8, "xs")
         xg = [tile([P, S], U32, "xg%d" % g) for g in range(PASSES)]
-        y = [ps.tile([P, S], F32, name="y%d" % t) for t in range(PACK)]
+        y = [ps.tile([P, S], F32, name="y%d" % t, tag="bank%d" % t) for t in range(PACK)]
         for g in range(PASSES):
             nc.vector.quantize_mx(
                 w1_codes[g][:].bitcast(FP8X4), w1_scales[g][:], w1_bf[g][:].rearrange("p t m j -> p (t m j)")
@@ -107,7 +105,7 @@ def tile_picked_anc8_silu_po_kernel(
             if g == 0:
                 nc.vector.tensor_copy(xs[:], xs_all[:].indirect(picked[:]))
             nc.vector.tensor_copy(xg[g][:], x_all[g][:].bitcast(U32).indirect(picked[:]))
-            for t in (2, 0, 3, 1):
+            for t in (2, 3, 0, 1):
                 cols = slice(t * P, (t + 1) * P)
                 nc.tensor.matmul_mx(
                     y[t][:],
@@ -119,116 +117,131 @@ def tile_picked_anc8_silu_po_kernel(
                     stop=(g == PASSES - 1),
                 )
 
-        e3.append(tile([P, S], F32, "e3_1", "x_all1"))
-        nc.vector.tensor_tensor(e3[1][:], table[1][:].indirect(lists[2][:]), e2[:, 1, :], ADD)
         w2_codes = tile([P, N], I32, "w2_codes")
         w2_sc = tile([P, N], U8, "w2_sc")
         nc.vector.tensor_copy(
             w2_codes[:].rearrange("p (t m) -> p m t", t=PACK), w2_raw[:].rearrange("p (m t) -> p m t", t=PACK)
         )
+        e3.append(tile([P, S], F32, "e3_1", "x_all1"))
+        nc.vector.tensor_tensor(e3[1][:], table[1][:].indirect(lists[2][:]), e2[:, 1, :], ADD)
         nc.vector.tensor_copy(
             w2_sc[:].rearrange("p (t m) -> p m t", t=PACK), w2s_raw[:].rearrange("p (m t) -> p m t", t=PACK)
         )
 
-        u = [tile([P, PACK, HALF], F32, "u0")]
-        y_sb = tile([P, PACK - EARLY, S], F32, "y_sb")
+        y_sb = [[tile([P, HALF], F32, "y_sb%d_%d" % (a, t)) for t in range(PACK - EARLY)] for a in range(2)]
+        for a in range(2):
+            for t in range(EARLY, PACK):
+                nc.scalar.copy(y_sb[a][t - EARLY][:], y[t][:, a * HALF : (a + 1) * HALF])
 
         out_rows = out_0.rearrange("(p t) j -> p t j", t=PACK)
         out_words = out_1[0].rearrange("p n t -> p (n t)").bitcast(I32)
         o_scales = tile([P, S], U8, "o_scales")
         state = {}
 
-        def activate(c):
+        def look_up(dst, t, lst, a, b, src):
+            nc.vector.tensor_tensor(dst, table[t][:].indirect(lst[:, a // 16 : b // 16]), src, ADD)
+
+        def first_two(r, a, b):
+            f1 = [tile([P, b - a], F32, "f1_%d_%d" % (r, t), "f%d_%d" % (r % 2, t)) for t in range(2)]
+            for t in range(2):
+                look_up(f1[t][:], 2 + t, lists[0], a, b, y_sb[a // HALF][t][:, a % HALF : a % HALF + b - a])
+            f2 = [tile([P, b - a], F32, "f2_%d_%d" % (r, t), "f%d_%d" % ((r + 1) % 2, t)) for t in range(2)]
+            for t in range(2):
+                look_up(f2[t][:], 2 + t, lists[1], a, b, f1[t][:])
+            state["f", r] = f2
+
+        def early_add(r, a, b):
+            u = tile([P, PACK, b - a], F32, "u%d" % r, "u")
+            for t in range(EARLY):
+                nc.vector.tensor_tensor(u[:, t, :], y[t][:, a:b], e3[t][:, a:b], ADD)
+            state["u", r] = u
+
+        def third(c, r, a):
+            cols = slice(c * PIECE - a, (c + 1) * PIECE - a)
+            for t in range(2):
+                look_up(state["u", r][:, 2 + t, cols], 2 + t, lists[2], c * PIECE, (c + 1) * PIECE, state["f", r][t][:, cols])
             z_bf = tile([P, PIECE, PACK], BF16, "z_bf%d" % c)
             nc.scalar.activation(
                 z_bf[:].rearrange("p (c i) t -> p c t i", i=4),
-                u[c // 2][:, :, c % 2 * PIECE : (c % 2 + 1) * PIECE].rearrange("p t (c i) -> p c t i", i=4),
+                state["u", r][:, :, cols].rearrange("p t (c i) -> p c t i", i=4),
                 SILU,
             )
             state["z", c] = z_bf
 
-        def second_layer(c):
+        def product(c, dst, t):
+            cols = slice(t * P, (t + 1) * P)
+            z_codes, z_scales = state["zq", c]
+            nc.tensor.matmul_mx(
+                dst,
+                lhsT=w2_codes[:, cols].bitcast(FP8X4),
+                lhsT_scale=w2_sc[:, cols],
+                rhs=z_codes[:].bitcast(FP8X4),
+                rhs_scale=z_scales[:],
+                start=True,
+                stop=True,
+            )
+
+        def quantise_z(c):
             z_codes = tile([P, PIECE], U32, "z_codes%d" % c)
             z_scales = tile([P, PIECE], U8, "z_scales%d" % c)
             nc.vector.quantize_mx(
                 z_codes[:].bitcast(FP8X4), z_scales[:], state["z", c][:].rearrange("p n t -> p (n t)")
             )
+            state["zq", c] = (z_codes, z_scales)
+
+        def second_layer(c, o_bf):
             acc = ps.tile([P, PACK, PIECE], F32, name="acc%d" % c)
             for t in range(PACK):
-                cols = slice(t * P, (t + 1) * P)
-                nc.tensor.matmul_mx(
-                    acc[:, t, :],
-                    lhsT=w2_codes[:, cols].bitcast(FP8X4),
-                    lhsT_scale=w2_sc[:, cols],
-                    rhs=z_codes[:].bitcast(FP8X4),
-                    rhs_scale=z_scales[:],
-                    start=True,
-                    stop=True,
-                )
+                product(c, acc[:, t, :], t)
             o_f32 = tile([P, PACK, PIECE], F32, "o_f32%d" % c)
-            o_bf = tile([P, PIECE, PACK], BF16, "o_bf%d" % c)
-            if c >= 2:
-                nc.scalar.copy(o_f32[:], acc[:])
-                nc.vector.tensor_copy(
-                    o_bf[:].rearrange("p (c i) t -> p c t i", i=4), o_f32[:].rearrange("p t (c i) -> p c t i", i=4)
-                )
-            else:
-                nc.scalar.copy(o_bf[:], acc[:].rearrange("p t n -> p n t"))
-                nc.scalar.copy(o_f32[:], acc[:])
+            nc.scalar.copy(o_f32[:], acc[:])
+            nc.scalar.copy(o_bf, acc[:].rearrange("p t n -> p n t"))
             nc.sync.dma_start(out_rows[:, :, c * PIECE : (c + 1) * PIECE], o_f32[:])
-            state["o", c] = o_bf
 
-        def hand_on(c):
-            cols = slice(c * PIECE, (c + 1) * PIECE)
-            o_codes = tile([P, PIECE], I32, "o_codes%d" % c)
+        def last_layer(c):
+            acc = [ps.tile([P, 2, PIECE], F32, name="last%d" % b, tag="bank%d" % (2 + b)) for b in range(2)]
+            for t in range(PACK):
+                product(c, acc[t // 2][:, t % 2, :], t)
+            o_f32 = [tile([P, 2, PIECE], F32, "last_f32%d" % b) for b in range(2)]
+            o_bf = tile([P, PIECE, PACK], BF16, "o_bf%d" % c)
+            nc.scalar.copy(o_f32[0][:], acc[0][:])
+            nc.vector.tensor_copy(o_bf[:, :, 2:4], acc[1][:].rearrange("p t n -> p n t"))
+            nc.vector.tensor_copy(o_bf[:, :, 0:2], acc[0][:].rearrange("p t n -> p n t"))
+            nc.scalar.copy(o_f32[1][:], acc[1][:])
+            for b in range(2):
+                nc.sync.dma_start(out_rows[:, 2 * b : 2 * b + 2, c * PIECE : (c + 1) * PIECE], o_f32[b][:])
+            return o_bf
+
+        def hand_on(a, b, o_bf, tag):
+            o_codes = tile([P, b - a], I32, "o_codes%d" % a, tag)
             nc.vector.quantize_mx(
-                o_codes[:].bitcast(FP8X4), o_scales[:, cols], state["o", c][:].rearrange("p n t -> p (n t)")
+                o_codes[:].bitcast(FP8X4), o_scales[:, a:b], o_bf[:].rearrange("p n t -> p (n t)")
             )
-            nc.sync.dma_start(out_words[:, cols], o_codes[:])
+            nc.sync.dma_start(out_words[:, a:b], o_codes[:])
 
-        def look_up(dst, t, lst, a, b, src):
-            nc.vector.tensor_tensor(dst, table[t][:].indirect(entries(lst, a, b)), src, ADD)
-
-        def early_add(a, b):
-            for t in range(EARLY):
-                nc.vector.tensor_tensor(u[a // HALF][:, t, :], y[t][:, a:b], e3[t][:, a:b], ADD)
-
-        for a in (0, HALF):
-            for t in range(EARLY, PACK):
-                nc.scalar.copy(y_sb[:, t - EARLY, a : a + HALF], y[t][:, a : a + HALF])
-        early_add(0, HALF)
-        f1 = [tile([P, HALF], F32, "f1_%d" % t) for t in range(2)]
-        f2 = [tile([P, HALF], F32, "f2_%d" % t) for t in range(2)]
-        for t in range(2):
-            look_up(f1[t][:], 2 + t, lists[0], 0, HALF, y_sb[:, t, :HALF])
-        for t in range(2):
-            look_up(f2[t][:], 2 + t, lists[1], 0, HALF, f1[t][:])
-        for t in range(2):
-            look_up(u[0][:, 2 + t, :], 2 + t, lists[2], 0, HALF, f2[t][:])
-        activate(0)
-        activate(1)
-        g1_2 = tile([P, HALF], F32, "g1_2", "f2_0")
-        look_up(g1_2[:], 2, lists[0], HALF, S, y_sb[:, 0, HALF:])
-        u.append(tile([P, PACK, HALF], F32, "u1", "f2_1"))
-        early_add(HALF, S)
-        second_layer(0)
-        g1_3 = tile([P, HALF], F32, "g1_3", "z_bf0")
-        look_up(g1_3[:], 3, lists[0], HALF, S, y_sb[:, 1, HALF:])
-        second_layer(1)
-        g2 = tile([P, 2, HALF], F32, "g2", "z_bf1")
-        look_up(g2[:, 0, :], 2, lists[1], HALF, S, g1_2[:])
-        look_up(g2[:, 1, :], 3, lists[1], HALF, S, g1_3[:])
-        for c in (2, 3):
-            for t in range(2):
-                a = c * PIECE
-                look_up(u[1][:, 2 + t, a - HALF : a - HALF + PIECE], 2 + t, lists[2], a, a + PIECE, g2[:, t, a - HALF : a - HALF + PIECE])
-            activate(c)
-        hand_on(0)
-        second_layer(2)
-        hand_on(1)
-        second_layer(3)
-        hand_on(2)
-        hand_on(3)
+        o_half = tile([P, HALF, PACK], BF16, "o_half")
+        o_two = tile([P, PIECE, PACK], BF16, "o_two")
+        first_two(0, 0, HALF)
+        early_add(0, 0, HALF)
+        third(0, 0, 0)
+        third(1, 0, 0)
+        quantise_z(0)
+        second_layer(0, o_half[:, :PIECE, :])
+        first_two(1, HALF, HALF + PIECE)
+        quantise_z(1)
+        early_add(1, HALF, HALF + PIECE)
+        third(2, 1, HALF)
+        second_layer(1, o_half[:, PIECE:, :])
+        first_two(2, HALF + PIECE, S)
+        quantise_z(2)
+        early_add(2, HALF + PIECE, S)
+        third(3, 2, HALF + PIECE)
+        second_layer(2, o_two[:])
+        quantise_z(3)
+        hand_on(0, HALF, o_half, "f1_0")
+        o_three = last_layer(3)
+        hand_on(HALF, HALF + PIECE, o_two, None)
+        hand_on(HALF + PIECE, S, o_three, None)
         for q in range(QUADS):
             queue = nc.sync if q % 2 else nc.scalar
             queue.dma_start(

@@ -105,17 +105,25 @@ def tile_picked_anc8_silu_po_kernel(
             if g == 0:
                 nc.vector.tensor_copy(xs[:], xs_all[:].indirect(picked[:]))
             nc.vector.tensor_copy(xg[g][:], x_all[g][:].bitcast(U32).indirect(picked[:]))
-            for t in (2, 3, 0, 1):
-                cols = slice(t * P, (t + 1) * P)
-                nc.tensor.matmul_mx(
-                    y[t][:],
-                    lhsT=w1_codes[g][:, cols].bitcast(FP8X4),
-                    lhsT_scale=w1_scales[g][:, cols],
-                    rhs=xg[g][:].bitcast(FP8X4),
-                    rhs_scale=xs[4 * g : P, :],
-                    start=(g == 0),
-                    stop=(g == PASSES - 1),
-                )
+
+        def first_layer(t, g, start):
+            cols = slice(t * P, (t + 1) * P)
+            nc.tensor.matmul_mx(
+                y[t][:],
+                lhsT=w1_codes[g][:, cols].bitcast(FP8X4),
+                lhsT_scale=w1_scales[g][:, cols],
+                rhs=xg[g][:].bitcast(FP8X4),
+                rhs_scale=xs[4 * g : P, :],
+                start=start,
+                stop=not start,
+            )
+
+        for g in range(PASSES):
+            for t in range(EARLY, PACK):
+                first_layer(t, g, g == 0)
+        for t in range(EARLY):
+            for g in reversed(range(PASSES)):
+                first_layer(t, g, g == PASSES - 1)
 
         w2_codes = tile([P, N], I32, "w2_codes")
         w2_sc = tile([P, N], U8, "w2_sc")
@@ -136,112 +144,108 @@ def tile_picked_anc8_silu_po_kernel(
         out_rows = out_0.rearrange("(p t) j -> p t j", t=PACK)
         out_words = out_1[0].rearrange("p n t -> p (n t)").bitcast(I32)
         o_scales = tile([P, S], U8, "o_scales")
-        state = {}
 
-        def look_up(dst, t, lst, a, b, src):
-            nc.vector.tensor_tensor(dst, table[t][:].indirect(lst[:, a // 16 : b // 16]), src, ADD)
+        def look_up(dst, t, n, a, b, src):
+            nc.vector.tensor_tensor(dst, table[t][:].indirect(lists[n][:, a // 16 : b // 16]), src, ADD)
 
-        def first_two(r, a, b):
-            f1 = [tile([P, b - a], F32, "f1_%d_%d" % (r, t), "f%d_%d" % (r % 2, t)) for t in range(2)]
+        u = [tile([P, PACK, HALF], F32, "u%d" % h) for h in range(2)]
+
+        def first(h):
+            f1 = [tile([P, HALF], F32, "f1_%d_%d" % (h, t), "f%d_%d" % (h, t)) for t in range(2)]
             for t in range(2):
-                look_up(f1[t][:], 2 + t, lists[0], a, b, y_sb[a // HALF][t][:, a % HALF : a % HALF + b - a])
-            f2 = [tile([P, b - a], F32, "f2_%d_%d" % (r, t), "f%d_%d" % ((r + 1) % 2, t)) for t in range(2)]
-            for t in range(2):
-                look_up(f2[t][:], 2 + t, lists[1], a, b, f1[t][:])
-            state["f", r] = f2
+                look_up(f1[t][:], EARLY + t, 0, h * HALF, (h + 1) * HALF, y_sb[h][t][:])
+            return f1
 
-        def early_add(r, a, b):
-            u = tile([P, PACK, b - a], F32, "u%d" % r, "u")
+        def early_add(h):
             for t in range(EARLY):
-                nc.vector.tensor_tensor(u[:, t, :], y[t][:, a:b], e3[t][:, a:b], ADD)
-            state["u", r] = u
+                cols = slice(h * HALF, (h + 1) * HALF)
+                nc.vector.tensor_tensor(u[h][:, t, :], y[t][:, cols], e3[t][:, cols], ADD)
 
-        def third(c, r, a):
-            cols = slice(c * PIECE - a, (c + 1) * PIECE - a)
+        def second(h, f1):
+            f2 = [tile([P, HALF], F32, "f2_%d_%d" % (h, t), "f%d_%d" % (1 - h, t)) for t in range(2)]
             for t in range(2):
-                look_up(state["u", r][:, 2 + t, cols], 2 + t, lists[2], c * PIECE, (c + 1) * PIECE, state["f", r][t][:, cols])
+                look_up(f2[t][:], EARLY + t, 1, h * HALF, (h + 1) * HALF, f1[t][:])
+            return f2
+
+        def third(h, f2, a, b):
+            for t in range(2):
+                look_up(u[h][:, EARLY + t, a:b], EARLY + t, 2, h * HALF + a, h * HALF + b, f2[t][:, a:b])
+
+        def activate(c):
             z_bf = tile([P, PIECE, PACK], BF16, "z_bf%d" % c)
             nc.scalar.activation(
                 z_bf[:].rearrange("p (c i) t -> p c t i", i=4),
-                state["u", r][:, :, cols].rearrange("p t (c i) -> p c t i", i=4),
+                u[c // 2][:, :, c % 2 * PIECE : (c % 2 + 1) * PIECE].rearrange("p t (c i) -> p c t i", i=4),
                 SILU,
             )
-            state["z", c] = z_bf
+            return z_bf
 
-        def product(c, dst, t):
+        def quantise_z(c, z_bf):
+            z_codes = tile([P, PIECE], U32, "z_codes%d" % c)
+            z_scales = tile([P, PIECE], U8, "z_scales%d" % c)
+            nc.vector.quantize_mx(z_codes[:].bitcast(FP8X4), z_scales[:], z_bf[:].rearrange("p n t -> p (n t)"))
+            return z_codes, z_scales
+
+        def product(dst, zq, t):
             cols = slice(t * P, (t + 1) * P)
-            z_codes, z_scales = state["zq", c]
             nc.tensor.matmul_mx(
                 dst,
                 lhsT=w2_codes[:, cols].bitcast(FP8X4),
                 lhsT_scale=w2_sc[:, cols],
-                rhs=z_codes[:].bitcast(FP8X4),
-                rhs_scale=z_scales[:],
+                rhs=zq[0][:].bitcast(FP8X4),
+                rhs_scale=zq[1][:],
                 start=True,
                 stop=True,
             )
 
-        def quantise_z(c):
-            z_codes = tile([P, PIECE], U32, "z_codes%d" % c)
-            z_scales = tile([P, PIECE], U8, "z_scales%d" % c)
-            nc.vector.quantize_mx(
-                z_codes[:].bitcast(FP8X4), z_scales[:], state["z", c][:].rearrange("p n t -> p (n t)")
-            )
-            state["zq", c] = (z_codes, z_scales)
-
-        def second_layer(c, o_bf):
-            acc = ps.tile([P, PACK, PIECE], F32, name="acc%d" % c)
-            for t in range(PACK):
-                product(c, acc[:, t, :], t)
+        def second_layer(c, zq, banks):
             o_f32 = tile([P, PACK, PIECE], F32, "o_f32%d" % c)
-            nc.scalar.copy(o_f32[:], acc[:])
-            nc.scalar.copy(o_bf, acc[:].rearrange("p t n -> p n t"))
+            per = PACK // len(banks)
+            for b, bank in enumerate(banks):
+                acc = ps.tile([P, per, PIECE], F32, name="acc%d_%d" % (c, b), tag=bank)
+                for t in range(per):
+                    product(acc[:, t, :], zq, b * per + t)
+                if c == 0:
+                    nc.scalar.copy(o_bf[0][:], acc[:].rearrange("p t n -> p n t"))
+                nc.scalar.copy(o_f32[:, b * per : (b + 1) * per, :], acc[:])
             nc.sync.dma_start(out_rows[:, :, c * PIECE : (c + 1) * PIECE], o_f32[:])
+            return o_f32
 
-        def last_layer(c):
-            acc = [ps.tile([P, 2, PIECE], F32, name="last%d" % b, tag="bank%d" % (2 + b)) for b in range(2)]
-            for t in range(PACK):
-                product(c, acc[t // 2][:, t % 2, :], t)
-            o_f32 = [tile([P, 2, PIECE], F32, "last_f32%d" % b) for b in range(2)]
-            o_bf = tile([P, PIECE, PACK], BF16, "o_bf%d" % c)
-            nc.scalar.copy(o_f32[0][:], acc[0][:])
-            nc.vector.tensor_copy(o_bf[:, :, 2:4], acc[1][:].rearrange("p t n -> p n t"))
-            nc.vector.tensor_copy(o_bf[:, :, 0:2], acc[0][:].rearrange("p t n -> p n t"))
-            nc.scalar.copy(o_f32[1][:], acc[1][:])
-            for b in range(2):
-                nc.sync.dma_start(out_rows[:, 2 * b : 2 * b + 2, c * PIECE : (c + 1) * PIECE], o_f32[b][:])
-            return o_bf
-
-        def hand_on(a, b, o_bf, tag):
-            o_codes = tile([P, b - a], I32, "o_codes%d" % a, tag)
-            nc.vector.quantize_mx(
-                o_codes[:].bitcast(FP8X4), o_scales[:, a:b], o_bf[:].rearrange("p n t -> p (n t)")
+        def round_out(dst, o_f32):
+            nc.vector.tensor_copy(
+                dst.rearrange("p (c i) t -> p c t i", i=4), o_f32[:].rearrange("p t (c i) -> p c t i", i=4)
             )
-            nc.sync.dma_start(out_words[:, a:b], o_codes[:])
 
-        o_half = tile([P, HALF, PACK], BF16, "o_half")
-        o_two = tile([P, PIECE, PACK], BF16, "o_two")
-        first_two(0, 0, HALF)
-        early_add(0, 0, HALF)
-        third(0, 0, 0)
-        third(1, 0, 0)
-        quantise_z(0)
-        second_layer(0, o_half[:, :PIECE, :])
-        first_two(1, HALF, HALF + PIECE)
-        quantise_z(1)
-        early_add(1, HALF, HALF + PIECE)
-        third(2, 1, HALF)
-        second_layer(1, o_half[:, PIECE:, :])
-        first_two(2, HALF + PIECE, S)
-        quantise_z(2)
-        early_add(2, HALF + PIECE, S)
-        third(3, 2, HALF + PIECE)
-        second_layer(2, o_two[:])
-        quantise_z(3)
-        hand_on(0, HALF, o_half, "f1_0")
-        o_three = last_layer(3)
-        hand_on(HALF, HALF + PIECE, o_two, None)
-        hand_on(HALF + PIECE, S, o_three, None)
+        def hand_on(a, src, tag):
+            cols = slice(a, a + src.shape[1])
+            o_codes = tile([P, src.shape[1]], I32, "o_codes%d" % a, tag)
+            nc.vector.quantize_mx(o_codes[:].bitcast(FP8X4), o_scales[:, cols], src[:].rearrange("p n t -> p (n t)"))
+            nc.sync.dma_start(out_words[:, cols], o_codes[:])
+
+        o_bf = [tile([P, PIECE, PACK], BF16, "o_bf0")]
+        f1 = first(0)
+        early_add(0)
+        third(0, second(0, f1), 0, HALF)
+        z = [activate(0), activate(1)]
+        o = [second_layer(c, quantise_z(c, z[c]), ["bank%d" % (4 + c)]) for c in range(2)]
+        f1 = first(1)
+        early_add(1)
+        f2 = second(1, f1)
+        for c in range(2):
+            third(1, f2, c * PIECE, (c + 1) * PIECE)
+            z.append(activate(2 + c))
+        hand_on(0, o_bf[0], "f0_0")
+        zq2 = quantise_z(2, z[2])
+        o_bf.append(tile([P, PIECE, PACK], BF16, "o_bf1", "z_bf2"))
+        round_out(o_bf[1][:], o[1])
+        zq3 = quantise_z(3, z[3])
+        hand_on(PIECE, o_bf[1], "z_bf3")
+        o.append(second_layer(2, zq2, ["bank6"]))
+        o.append(second_layer(3, zq3, ["bank2", "bank3"]))
+        o_last = tile([P, HALF, PACK], BF16, "o_last")
+        for c in range(2):
+            round_out(o_last[:, c * PIECE : (c + 1) * PIECE, :], o[2 + c])
+        hand_on(HALF, o_last, None)
         for q in range(QUADS):
             queue = nc.sync if q % 2 else nc.scalar
             queue.dma_start(

@@ -44,15 +44,9 @@ def tile_picked_anc8_silu_po_kernel(
         xs_all = tile([P, T], U8, "xs_all")
         w2_raw = tile([P, N], I32, "w2_raw")
         w2s_raw = tile([P, N], U8, "w2s_raw")
-        warm = tile([P, 1], F32, "warm")
-        warm2 = tile([P, 1], F32, "warm2")
 
         nc.gpsimd.memset(xs_all[:].bitcast(I32), 0)
         nc.gpsimd.memset(w2s_raw[:].bitcast(I32), 0)
-        nc.gpsimd.memset(warm[:], 0.0)
-        for t in range(EARLY):
-            nc.vector.memset(table[t][:, U:], 0.0)
-        nc.scalar.activation(warm2[:], warm[:], SILU)
 
         emb_rows = emb.rearrange("(p t) u -> t p u", t=PACK)
         w1_rows = w1.rearrange("(g p j) c -> g p j c", p=P, j=PACK)
@@ -80,66 +74,82 @@ def tile_picked_anc8_silu_po_kernel(
 
         e1 = tile([P, EARLY, S], F32, "e1")
         e2 = tile([P, EARLY, S], F32, "e2")
-        e3 = [tile([P, S], F32, "e3_0")]
+        e3 = tile([P, EARLY, S], F32, "e3")
         for t in range(EARLY):
             nc.vector.tensor_copy(e1[:, t, :], table[t][:].indirect(lists[0][:]))
         for t in range(EARLY):
             nc.vector.tensor_tensor(e2[:, t, :], table[t][:].indirect(lists[1][:]), e1[:, t, :], ADD)
-        nc.vector.tensor_tensor(e3[0][:], table[0][:].indirect(lists[2][:]), e2[:, 0, :], ADD)
-
-        w1_codes, w1_scales = [], []
-        w1_bf = [tile([P, PACK, P, PACK], BF16, "w1_bf%d" % g) for g in range(PASSES)]
-        for g in range(PASSES):
-            nc.scalar.copy(
-                w1_bf[g][:].rearrange("p t m j -> p m j t"), w1_raw[g][:].rearrange("p j (m t) -> p m j t", t=PACK)
-            )
-            w1_codes.append(tile([P, H], U32, "w1_codes%d" % g))
-            w1_scales.append(tile([P, H], U8, "w1_scales%d" % g))
-        xs = tile([P, S], U8, "xs")
-        xg = [tile([P, S], U32, "xg%d" % g) for g in range(PASSES)]
-        y = [ps.tile([P, S], F32, name="y%d" % t, tag="bank%d" % t) for t in range(PACK)]
-        for g in range(PASSES):
-            nc.vector.quantize_mx(
-                w1_codes[g][:].bitcast(FP8X4), w1_scales[g][:], w1_bf[g][:].rearrange("p t m j -> p (t m j)")
-            )
-            if g == 0:
-                nc.vector.tensor_copy(xs[:], xs_all[:].indirect(picked[:]))
-            nc.vector.tensor_copy(xg[g][:], x_all[g][:].bitcast(U32).indirect(picked[:]))
-
-        def first_layer(t, g, start):
-            cols = slice(t * P, (t + 1) * P)
-            nc.tensor.matmul_mx(
-                y[t][:],
-                lhsT=w1_codes[g][:, cols].bitcast(FP8X4),
-                lhsT_scale=w1_scales[g][:, cols],
-                rhs=xg[g][:].bitcast(FP8X4),
-                rhs_scale=xs[4 * g : P, :],
-                start=start,
-                stop=not start,
-            )
-
-        for g in range(PASSES):
-            for t in range(EARLY, PACK):
-                first_layer(t, g, g == 0)
         for t in range(EARLY):
-            for g in reversed(range(PASSES)):
-                first_layer(t, g, g == PASSES - 1)
+            nc.vector.tensor_tensor(e3[:, t, :], table[t][:].indirect(lists[2][:]), e2[:, t, :], ADD)
 
+        def round_w1(g, a, b):
+            w1_bf = tile([P, b - a, P, PACK], BF16, "w1_bf%d_%d" % (g, a))
+            nc.scalar.copy(
+                w1_bf[:].rearrange("p t m j -> p m j t"),
+                w1_raw[g][:].rearrange("p j (m t) -> p m j t", t=PACK)[:, :, :, a:b],
+            )
+            return w1_bf
+
+        w1q = {}
+
+        def quantise_w1(g, a, w1_bf, tag):
+            width = w1_bf.shape[1] * P
+            codes = tile([P, width], U32, "w1_codes%d_%d" % (g, a), tag)
+            scales = tile([P, width], U8, "w1_scales%d_%d" % (g, a))
+            nc.vector.quantize_mx(codes[:].bitcast(FP8X4), scales[:], w1_bf[:].rearrange("p t m j -> p (t m j)"))
+            for t in range(w1_bf.shape[1]):
+                w1q[g, a + t] = (codes[:, t * P : (t + 1) * P], scales[:, t * P : (t + 1) * P])
+
+        xs = tile([P, S], U8, "xs")
+        xg0 = tile([P, S], U32, "xg0")
+        xg1 = [tile([P, HALF], U32, "xg1_%d" % h) for h in range(2)]
+        quantise_w1(0, 0, round_w1(0, 0, PACK), None)
+        nc.vector.tensor_copy(xs[:], xs_all[:].indirect(picked[:]))
+        quantise_w1(1, EARLY, round_w1(1, EARLY, PACK), None)
+        nc.vector.tensor_copy(xg0[:], x_all[0][:].bitcast(U32).indirect(picked[:]))
+        for h in range(2):
+            nc.vector.tensor_copy(
+                xg1[h][:], x_all[1][:].bitcast(U32).indirect(picked[:, h * HALF // 16 : (h + 1) * HALF // 16])
+            )
         w2_codes = tile([P, N], I32, "w2_codes")
         w2_sc = tile([P, N], U8, "w2_sc")
         nc.vector.tensor_copy(
             w2_codes[:].rearrange("p (t m) -> p m t", t=PACK), w2_raw[:].rearrange("p (m t) -> p m t", t=PACK)
         )
-        e3.append(tile([P, S], F32, "e3_1", "x_all1"))
-        nc.vector.tensor_tensor(e3[1][:], table[1][:].indirect(lists[2][:]), e2[:, 1, :], ADD)
-        nc.vector.tensor_copy(
-            w2_sc[:].rearrange("p (t m) -> p m t", t=PACK), w2s_raw[:].rearrange("p (m t) -> p m t", t=PACK)
-        )
+        quantise_w1(1, 0, round_w1(1, 0, EARLY), "x_all1")
+
+        def first_layer(dst, t, g, h, start):
+            half = slice(h * HALF, (h + 1) * HALF)
+            nc.tensor.matmul_mx(
+                dst,
+                lhsT=w1q[g, t][0].bitcast(FP8X4),
+                lhsT_scale=w1q[g, t][1],
+                rhs=(xg1[h][:] if g else xg0[:, half]).bitcast(FP8X4),
+                rhs_scale=xs[4 * g : P, half],
+                start=start,
+                stop=not start,
+            )
+
+        y_late = [
+            [ps.tile([P, HALF], F32, name="y%d_%d" % (h, t), tag="bank%d" % (2 * h + t)) for t in range(2)]
+            for h in range(2)
+        ]
+        y_early = [ps.tile([P, EARLY, HALF], F32, name="ye%d" % h, tag="bank%d" % (4 + h)) for h in range(2)]
+        for g in range(PASSES):
+            for t in range(2):
+                first_layer(y_late[0][t][:], EARLY + t, g, 0, g == 0)
+        for t in range(2):
+            for g in reversed(range(PASSES)):
+                first_layer(y_late[1][t][:], EARLY + t, g, 1, g == PASSES - 1)
+        for h in range(2):
+            for t in range(EARLY):
+                for g in reversed(range(PASSES)):
+                    first_layer(y_early[h][:, t, :], t, g, h, g == PASSES - 1)
 
         y_sb = [[tile([P, HALF], F32, "y_sb%d_%d" % (a, t)) for t in range(PACK - EARLY)] for a in range(2)]
-        for a in range(2):
-            for t in range(EARLY, PACK):
-                nc.scalar.copy(y_sb[a][t - EARLY][:], y[t][:, a * HALF : (a + 1) * HALF])
+        for h in range(2):
+            for t in range(2):
+                nc.scalar.copy(y_sb[h][t][:], y_late[h][t][:])
 
         out_rows = out_0.rearrange("(p t) j -> p t j", t=PACK)
         out_words = out_1[0].rearrange("p n t -> p (n t)").bitcast(I32)
@@ -157,9 +167,7 @@ def tile_picked_anc8_silu_po_kernel(
             return f1
 
         def early_add(h):
-            for t in range(EARLY):
-                cols = slice(h * HALF, (h + 1) * HALF)
-                nc.vector.tensor_tensor(u[h][:, t, :], y[t][:, cols], e3[t][:, cols], ADD)
+            nc.vector.tensor_tensor(u[h][:, :EARLY, :], y_early[h][:], e3[:, :, h * HALF : (h + 1) * HALF], ADD)
 
         def second(h, f1):
             f2 = [tile([P, HALF], F32, "f2_%d_%d" % (h, t), "f%d_%d" % (1 - h, t)) for t in range(2)]
@@ -224,10 +232,13 @@ def tile_picked_anc8_silu_po_kernel(
 
         o_bf = [tile([P, PIECE, PACK], BF16, "o_bf0")]
         f1 = first(0)
+        nc.vector.tensor_copy(
+            w2_sc[:].rearrange("p (t m) -> p m t", t=PACK), w2s_raw[:].rearrange("p (m t) -> p m t", t=PACK)
+        )
         early_add(0)
         third(0, second(0, f1), 0, HALF)
         z = [activate(0), activate(1)]
-        o = [second_layer(c, quantise_z(c, z[c]), ["bank%d" % (4 + c)]) for c in range(2)]
+        o = [second_layer(c, quantise_z(c, z[c]), ["bank%d" % (6 + c)]) for c in range(2)]
         f1 = first(1)
         early_add(1)
         f2 = second(1, f1)
@@ -240,11 +251,14 @@ def tile_picked_anc8_silu_po_kernel(
         round_out(o_bf[1][:], o[1])
         zq3 = quantise_z(3, z[3])
         hand_on(PIECE, o_bf[1], "z_bf3")
-        o.append(second_layer(2, zq2, ["bank6"]))
-        o.append(second_layer(3, zq3, ["bank2", "bank3"]))
+        o.append(second_layer(2, zq2, ["bank0"]))
         o_last = tile([P, HALF, PACK], BF16, "o_last")
-        for c in range(2):
-            round_out(o_last[:, c * PIECE : (c + 1) * PIECE, :], o[2 + c])
+        round_out(o_last[:, :PIECE, :], o[2])
+        twin = ps.tile([P, PACK, PIECE], F32, name="twin", tag="bank1")
+        for t in range(PACK):
+            product(twin[:, t, :], zq3, t)
+        nc.vector.tensor_copy(o_last[:, PIECE:, :], twin[:].rearrange("p t n -> p n t"))
+        second_layer(3, zq3, ["bank2", "bank3"])
         hand_on(HALF, o_last, None)
         for q in range(QUADS):
             queue = nc.sync if q % 2 else nc.scalar

@@ -1,6 +1,7 @@
 from contextlib import ExitStack
 
 import concourse.mybir as mybir
+from concourse.masks import make_identity
 
 K, T, S, N, H, U = 1024, 2048, 512, 512, 512, 512
 FLOPS = 2 * K * H * S + 2 * H * N * S
@@ -47,6 +48,8 @@ def tile_picked_anc8_silu_po_kernel(
 
         nc.gpsimd.memset(xs_all[:].bitcast(I32), 0)
         nc.gpsimd.memset(w2s_raw[:].bitcast(I32), 0)
+        ident = tile([P, P], F32, "ident")
+        make_identity(nc, ident[:])
 
         emb_rows = emb.rearrange("(p t) u -> t p u", t=PACK)
         w1_rows = w1.rearrange("(g p j) c -> g p j c", p=P, j=PACK)
@@ -65,12 +68,12 @@ def tile_picked_anc8_silu_po_kernel(
         for g in range(PASSES):
             nc.sync.dma_start(x_all[g][:], x_words[g].rearrange("p n t -> p (n t)").bitcast(I32))
         nc.sync.dma_start(w2_raw[:], w2_words[0].rearrange("p n t -> p (n t)").bitcast(I32))
-        nc.sync.dma_start(table[2][:], emb_rows[2])
-        nc.sync.dma_start(table[3][:], emb_rows[3])
         for q in range(QUADS):
             nc.sync.dma_start(
                 w2s_raw[32 * q : 32 * q + 4, :].bitcast(I32), w2_scales[0, 4 * q : 4 * q + 4, :].bitcast(I32)
             )
+        nc.sync.dma_start(table[2][:], emb_rows[2])
+        nc.sync.dma_start(table[3][:], emb_rows[3])
 
         e1 = tile([P, EARLY, S], F32, "e1")
         e2 = tile([P, EARLY, S], F32, "e2")
@@ -82,6 +85,16 @@ def tile_picked_anc8_silu_po_kernel(
         for t in range(EARLY):
             nc.vector.tensor_tensor(e3[:, t, :], table[t][:].indirect(lists[2][:]), e2[:, t, :], ADD)
 
+        e_turned = []
+        for h in range(2):
+            e_ps = ps.tile([P, 2, EARLY, P], F32, name="e_ps%d" % h, tag="bank%d" % (4 + h))
+            for c in range(2):
+                for t in range(EARLY):
+                    nc.tensor.transpose(
+                        e_ps[:, c, t, :], e3[:, t, h * HALF + c * P : h * HALF + (c + 1) * P], ident[:]
+                    )
+            e_turned.append(e_ps)
+
         def round_w1(g, a, b):
             w1_bf = tile([P, b - a, P, PACK], BF16, "w1_bf%d_%d" % (g, a))
             nc.scalar.copy(
@@ -91,12 +104,15 @@ def tile_picked_anc8_silu_po_kernel(
             return w1_bf
 
         w1q = {}
+        w1_early = {}
 
         def quantise_w1(g, a, w1_bf, tag):
             width = w1_bf.shape[1] * P
             codes = tile([P, width], U32, "w1_codes%d_%d" % (g, a), tag)
             scales = tile([P, width], U8, "w1_scales%d_%d" % (g, a))
             nc.vector.quantize_mx(codes[:].bitcast(FP8X4), scales[:], w1_bf[:].rearrange("p t m j -> p (t m j)"))
+            if a == 0:
+                w1_early[g] = (codes[:, : EARLY * P], scales[:, : EARLY * P])
             for t in range(w1_bf.shape[1]):
                 w1q[g, a + t] = (codes[:, t * P : (t + 1) * P], scales[:, t * P : (t + 1) * P])
 
@@ -118,6 +134,25 @@ def tile_picked_anc8_silu_po_kernel(
         )
         quantise_w1(1, 0, round_w1(1, 0, EARLY), "x_all1")
 
+        u_ps = [ps.tile([P, EARLY, HALF], F32, name="u_ps%d" % h, tag="bank%d" % (6 + h)) for h in range(2)]
+
+        def turn_back(h, src, first):
+            for c in range(2):
+                for t in range(EARLY):
+                    nc.tensor.matmul(
+                        u_ps[h][:, t, c * P : (c + 1) * P],
+                        lhsT=src[:, c, t, :],
+                        rhs=ident[:],
+                        is_transpose=True,
+                        start=first and c == 0 and t == 0,
+                        stop=not first and c == 1 and t == EARLY - 1,
+                    )
+
+        e_sb = tile([P, 2, 2, EARLY, P], F32, "e_sb", "w1_raw1")
+        for h in range(2):
+            nc.scalar.copy(e_sb[:, h], e_turned[h][:])
+            turn_back(h, e_sb[:, h], True)
+
         def first_layer(dst, t, g, h, start):
             half = slice(h * HALF, (h + 1) * HALF)
             nc.tensor.matmul_mx(
@@ -134,7 +169,7 @@ def tile_picked_anc8_silu_po_kernel(
             [ps.tile([P, HALF], F32, name="y%d_%d" % (h, t), tag="bank%d" % (2 * h + t)) for t in range(2)]
             for h in range(2)
         ]
-        y_early = [ps.tile([P, EARLY, HALF], F32, name="ye%d" % h, tag="bank%d" % (4 + h)) for h in range(2)]
+        y_early = [ps.tile([P, 2, EARLY, P], F32, name="ye%d" % h, tag="bank%d" % (4 + h)) for h in range(2)]
         for g in range(PASSES):
             for t in range(2):
                 first_layer(y_late[0][t][:], EARLY + t, g, 0, g == 0)
@@ -142,9 +177,18 @@ def tile_picked_anc8_silu_po_kernel(
             for g in reversed(range(PASSES)):
                 first_layer(y_late[1][t][:], EARLY + t, g, 1, g == PASSES - 1)
         for h in range(2):
-            for t in range(EARLY):
+            for c in range(2):
+                cols = slice(h * HALF + c * P, h * HALF + (c + 1) * P)
                 for g in reversed(range(PASSES)):
-                    first_layer(y_early[h][:, t, :], t, g, h, g == PASSES - 1)
+                    nc.tensor.matmul_mx(
+                        y_early[h][:, c, :, :].rearrange("p t m -> p (t m)"),
+                        lhsT=(xg1[h][:, c * P : (c + 1) * P] if g else xg0[:, cols]).bitcast(FP8X4),
+                        lhsT_scale=xs[4 * g : P, cols],
+                        rhs=w1_early[g][0].bitcast(FP8X4),
+                        rhs_scale=w1_early[g][1],
+                        start=g == PASSES - 1,
+                        stop=g == 0,
+                    )
 
         y_sb = [[tile([P, HALF], F32, "y_sb%d_%d" % (a, t)) for t in range(PACK - EARLY)] for a in range(2)]
         for h in range(2):
@@ -158,63 +202,54 @@ def tile_picked_anc8_silu_po_kernel(
         def look_up(dst, t, n, a, b, src):
             nc.vector.tensor_tensor(dst, table[t][:].indirect(lists[n][:, a // 16 : b // 16]), src, ADD)
 
-        u = [tile([P, PACK, HALF], F32, "u%d" % h) for h in range(2)]
+        z_first = tile([P, HALF, PACK], BF16, "z_first")
+        z = [tile([P, PIECE, PACK], BF16, "z_bf%d" % c) for c in range(2)]
 
-        def first(h):
-            f1 = [tile([P, HALF], F32, "f1_%d_%d" % (h, t), "f%d_%d" % (h, t)) for t in range(2)]
+        def chain(n, a, b, src):
+            dst = [tile([P, b - a], F32, "f%d_%d_%d" % (n, a, t), "f%d_%d" % (n, t)) for t in range(2)]
             for t in range(2):
-                look_up(f1[t][:], EARLY + t, 0, h * HALF, (h + 1) * HALF, y_sb[h][t][:])
-            return f1
+                look_up(dst[t][:], EARLY + t, n, a, b, src[t])
+            return [d[:] for d in dst]
 
-        def early_add(h):
-            nc.vector.tensor_tensor(u[h][:, :EARLY, :], y_early[h][:], e3[:, :, h * HALF : (h + 1) * HALF], ADD)
-
-        def second(h, f1):
-            f2 = [tile([P, HALF], F32, "f2_%d_%d" % (h, t), "f%d_%d" % (1 - h, t)) for t in range(2)]
+        def third(u, f2, a, b):
             for t in range(2):
-                look_up(f2[t][:], EARLY + t, 1, h * HALF, (h + 1) * HALF, f1[t][:])
-            return f2
+                look_up(u[:, t, :], EARLY + t, 2, a, b, f2[t])
 
-        def third(h, f2, a, b):
-            for t in range(2):
-                look_up(u[h][:, EARLY + t, a:b], EARLY + t, 2, h * HALF + a, h * HALF + b, f2[t][:, a:b])
-
-        def activate(c):
-            z_bf = tile([P, PIECE, PACK], BF16, "z_bf%d" % c)
+        def activate(dst, src):
             nc.scalar.activation(
-                z_bf[:].rearrange("p (c i) t -> p c t i", i=4),
-                u[c // 2][:, :, c % 2 * PIECE : (c % 2 + 1) * PIECE].rearrange("p t (c i) -> p c t i", i=4),
-                SILU,
+                dst.rearrange("p (c i) t -> p c t i", i=4), src.rearrange("p t (c i) -> p c t i", i=4), SILU
             )
-            return z_bf
 
-        def quantise_z(c, z_bf):
-            z_codes = tile([P, PIECE], U32, "z_codes%d" % c)
-            z_scales = tile([P, PIECE], U8, "z_scales%d" % c)
+        def add_y(h):
+            y_turned = tile([P, 2, EARLY, P], F32, "y_turned%d" % h)
+            nc.scalar.copy(y_turned[:], y_early[h][:])
+            turn_back(h, y_turned, False)
+
+        def quantise_z(name, z_bf):
+            z_codes = tile([P, z_bf.shape[1]], U32, name + "_codes")
+            z_scales = tile([P, z_bf.shape[1]], U8, name + "_scales")
             nc.vector.quantize_mx(z_codes[:].bitcast(FP8X4), z_scales[:], z_bf[:].rearrange("p n t -> p (n t)"))
             return z_codes, z_scales
 
-        def product(dst, zq, t):
-            cols = slice(t * P, (t + 1) * P)
-            nc.tensor.matmul_mx(
-                dst,
-                lhsT=w2_codes[:, cols].bitcast(FP8X4),
-                lhsT_scale=w2_sc[:, cols],
-                rhs=zq[0][:].bitcast(FP8X4),
-                rhs_scale=zq[1][:],
-                start=True,
-                stop=True,
-            )
+        def second_layer(name, zq, a, planes, bank):
+            acc = ps.tile([P, len(planes), PIECE], F32, name=name, tag=bank)
+            for n, t in enumerate(planes):
+                cols = slice(t * P, (t + 1) * P)
+                nc.tensor.matmul_mx(
+                    acc[:, n, :],
+                    lhsT=w2_codes[:, cols].bitcast(FP8X4),
+                    lhsT_scale=w2_sc[:, cols],
+                    rhs=zq[0][:, a : a + PIECE].bitcast(FP8X4),
+                    rhs_scale=zq[1][:, a : a + PIECE],
+                    start=True,
+                    stop=True,
+                )
+            return acc
 
-        def second_layer(c, zq, banks):
-            o_f32 = tile([P, PACK, PIECE], F32, "o_f32%d" % c)
-            per = PACK // len(banks)
-            for b, bank in enumerate(banks):
-                acc = ps.tile([P, per, PIECE], F32, name="acc%d_%d" % (c, b), tag=bank)
-                for t in range(per):
-                    product(acc[:, t, :], zq, b * per + t)
-                if c == 0:
-                    nc.scalar.copy(o_bf[0][:], acc[:].rearrange("p t n -> p n t"))
+        def store(c, accs, tag=None):
+            o_f32 = tile([P, PACK, PIECE], F32, "o_f32%d" % c, tag)
+            per = PACK // len(accs)
+            for b, acc in enumerate(accs):
                 nc.scalar.copy(o_f32[:, b * per : (b + 1) * per, :], acc[:])
             nc.sync.dma_start(out_rows[:, :, c * PIECE : (c + 1) * PIECE], o_f32[:])
             return o_f32
@@ -224,42 +259,51 @@ def tile_picked_anc8_silu_po_kernel(
                 dst.rearrange("p (c i) t -> p c t i", i=4), o_f32[:].rearrange("p t (c i) -> p c t i", i=4)
             )
 
-        def hand_on(a, src, tag):
+        def hand_on(a, src, tag=None):
             cols = slice(a, a + src.shape[1])
             o_codes = tile([P, src.shape[1]], I32, "o_codes%d" % a, tag)
             nc.vector.quantize_mx(o_codes[:].bitcast(FP8X4), o_scales[:, cols], src[:].rearrange("p n t -> p (n t)"))
             nc.sync.dma_start(out_words[:, cols], o_codes[:])
 
-        o_bf = [tile([P, PIECE, PACK], BF16, "o_bf0")]
-        f1 = first(0)
         nc.vector.tensor_copy(
             w2_sc[:].rearrange("p (t m) -> p m t", t=PACK), w2s_raw[:].rearrange("p (m t) -> p m t", t=PACK)
         )
-        early_add(0)
-        third(0, second(0, f1), 0, HALF)
-        z = [activate(0), activate(1)]
-        o = [second_layer(c, quantise_z(c, z[c]), ["bank%d" % (6 + c)]) for c in range(2)]
-        f1 = first(1)
-        early_add(1)
-        f2 = second(1, f1)
+        f1 = chain(0, 0, HALF, [y_sb[0][t][:] for t in range(2)])
+        add_y(0)
+        activate(z_first[:, :, :EARLY], u_ps[0][:])
+        u = tile([P, PACK - EARLY, HALF], F32, "u_first", "u")
+        third(u, chain(1, 0, HALF, f1), 0, HALF)
+        add_y(1)
         for c in range(2):
-            third(1, f2, c * PIECE, (c + 1) * PIECE)
-            z.append(activate(2 + c))
-        hand_on(0, o_bf[0], "f0_0")
-        zq2 = quantise_z(2, z[2])
-        o_bf.append(tile([P, PIECE, PACK], BF16, "o_bf1", "z_bf2"))
-        round_out(o_bf[1][:], o[1])
-        zq3 = quantise_z(3, z[3])
-        hand_on(PIECE, o_bf[1], "z_bf3")
-        o.append(second_layer(2, zq2, ["bank0"]))
+            activate(z[c][:, :, :EARLY], u_ps[1][:, :, c * PIECE : (c + 1) * PIECE])
+        activate(z_first[:, :, EARLY:], u[:])
+
+        def late_piece(c, between):
+            a, b = HALF + c * PIECE, HALF + (c + 1) * PIECE
+            f1 = chain(0, a, b, [y_sb[1][t][:, c * PIECE : (c + 1) * PIECE] for t in range(2)])
+            f2 = chain(1, a, b, f1)
+            made = between()
+            u = tile([P, PACK - EARLY, PIECE], F32, "u%d" % c, "u")
+            third(u, f2, a, b)
+            activate(z[c][:, :, EARLY:], u[:])
+            return made, u
+
+        zq, u = late_piece(0, lambda: quantise_z("z_first", z_first))
+        o = [store(c, [second_layer("acc%d" % c, zq, c * PIECE, range(PACK), "bank%d" % c)]) for c in range(2)]
+        zq, u = late_piece(1, lambda: quantise_z("z2", z[0]))
+        acc2 = second_layer("acc2", zq, 0, range(PACK), "bank4")
+        zq = quantise_z("z3", z[1])
+        twin = second_layer("twin", zq, 0, range(PACK), "bank5")
+        last = [second_layer("acc3_%d" % b, zq, 0, range(2 * b, 2 * b + 2), "bank%d" % (2 + b)) for b in range(2)]
+        o_first = tile([P, HALF, PACK], BF16, "o_first", "f1_0")
+        for c in range(2):
+            round_out(o_first[:, c * PIECE : (c + 1) * PIECE, :], o[c])
+        hand_on(0, o_first)
         o_last = tile([P, HALF, PACK], BF16, "o_last")
-        round_out(o_last[:, :PIECE, :], o[2])
-        twin = ps.tile([P, PACK, PIECE], F32, name="twin", tag="bank1")
-        for t in range(PACK):
-            product(twin[:, t, :], zq3, t)
+        round_out(o_last[:, :PIECE, :], store(2, [acc2]))
         nc.vector.tensor_copy(o_last[:, PIECE:, :], twin[:].rearrange("p t n -> p n t"))
-        second_layer(3, zq3, ["bank2", "bank3"])
-        hand_on(HALF, o_last, None)
+        store(3, last)
+        hand_on(HALF, o_last)
         for q in range(QUADS):
             queue = nc.sync if q % 2 else nc.scalar
             queue.dma_start(

@@ -32,6 +32,7 @@ def tile_picked_anc8_silu_po_kernel(
     nc = tc.nc
     with ExitStack() as ctx:
         sb = ctx.enter_context(tc.tile_pool(name="sb", bufs=1))
+        relay = ctx.enter_context(tc.tile_pool(name="relay", bufs=1))
         ps = ctx.enter_context(tc.psum_pool(name="ps", bufs=1))
 
         def tile(shape, dtype, name, tag=None):
@@ -203,7 +204,6 @@ def tile_picked_anc8_silu_po_kernel(
             nc.vector.tensor_tensor(dst, table[t][:].indirect(lists[n][:, a // 16 : b // 16]), src, ADD)
 
         z_first = tile([P, HALF, PACK], BF16, "z_first")
-        z = [tile([P, PIECE, PACK], BF16, "z_bf%d" % c) for c in range(2)]
 
         def chain(n, a, b, src):
             dst = [tile([P, b - a], F32, "f%d_%d_%d" % (n, a, t), "f%d_%d" % (n, t)) for t in range(2)]
@@ -228,7 +228,7 @@ def tile_picked_anc8_silu_po_kernel(
         def quantise_z(name, z_bf):
             z_codes = tile([P, z_bf.shape[1]], U32, name + "_codes")
             z_scales = tile([P, z_bf.shape[1]], U8, name + "_scales")
-            nc.vector.quantize_mx(z_codes[:].bitcast(FP8X4), z_scales[:], z_bf[:].rearrange("p n t -> p (n t)"))
+            nc.vector.quantize_mx(z_codes[:].bitcast(FP8X4), z_scales[:], z_bf.rearrange("p n t -> p (n t)"))
             return z_codes, z_scales
 
         def second_layer(name, zq, a, planes, bank):
@@ -246,12 +246,12 @@ def tile_picked_anc8_silu_po_kernel(
                 )
             return acc
 
-        def store(c, accs, tag=None):
-            o_f32 = tile([P, PACK, PIECE], F32, "o_f32%d" % c, tag)
+        def store(c, accs, queue=nc.sync):
+            o_f32 = tile([P, PACK, PIECE], F32, "o_f32%d" % c)
             per = PACK // len(accs)
             for b, acc in enumerate(accs):
                 nc.scalar.copy(o_f32[:, b * per : (b + 1) * per, :], acc[:])
-            nc.sync.dma_start(out_rows[:, :, c * PIECE : (c + 1) * PIECE], o_f32[:])
+            queue.dma_start(out_rows[:, :, c * PIECE : (c + 1) * PIECE], o_f32[:])
             return o_f32
 
         def round_out(dst, o_f32):
@@ -271,24 +271,25 @@ def tile_picked_anc8_silu_po_kernel(
         f1 = chain(0, 0, HALF, [y_sb[0][t][:] for t in range(2)])
         add_y(0)
         activate(z_first[:, :, :EARLY], u_ps[0][:])
-        u = tile([P, PACK - EARLY, HALF], F32, "u_first", "u")
+        u = relay.tile([P, PACK - EARLY, HALF], F32, name="u_first", offset=1024, align_bytes=64)
         third(u, chain(1, 0, HALF, f1), 0, HALF)
         add_y(1)
-        for c in range(2):
-            activate(z[c][:, :, :EARLY], u_ps[1][:, :, c * PIECE : (c + 1) * PIECE])
         activate(z_first[:, :, EARLY:], u[:])
+        z_second = relay.tile([P, HALF, PACK], BF16, name="z_second", offset=2048, align_bytes=64)
+        z = [z_second[:, c * PIECE : (c + 1) * PIECE, :] for c in range(2)]
+        activate(z_second[:, :, :EARLY], u_ps[1][:])
 
         def late_piece(c, between):
             a, b = HALF + c * PIECE, HALF + (c + 1) * PIECE
             f1 = chain(0, a, b, [y_sb[1][t][:, c * PIECE : (c + 1) * PIECE] for t in range(2)])
             f2 = chain(1, a, b, f1)
             made = between()
-            u = tile([P, PACK - EARLY, PIECE], F32, "u%d" % c, "u")
+            u = relay.tile([P, PACK - EARLY, PIECE], F32, name="u%d" % c, offset=512 - 512 * c, align_bytes=64)
             third(u, f2, a, b)
             activate(z[c][:, :, EARLY:], u[:])
             return made, u
 
-        zq, u = late_piece(0, lambda: quantise_z("z_first", z_first))
+        zq, u = late_piece(0, lambda: quantise_z("z_first", z_first[:]))
         o = [store(c, [second_layer("acc%d" % c, zq, c * PIECE, range(PACK), "bank%d" % c)]) for c in range(2)]
         zq, u = late_piece(1, lambda: quantise_z("z2", z[0]))
         acc2 = second_layer("acc2", zq, 0, range(PACK), "bank4")
@@ -299,11 +300,12 @@ def tile_picked_anc8_silu_po_kernel(
         for c in range(2):
             round_out(o_first[:, c * PIECE : (c + 1) * PIECE, :], o[c])
         hand_on(0, o_first)
-        o_last = tile([P, HALF, PACK], BF16, "o_last")
-        round_out(o_last[:, :PIECE, :], store(2, [acc2]))
-        nc.vector.tensor_copy(o_last[:, PIECE:, :], twin[:].rearrange("p t n -> p n t"))
-        store(3, last)
-        hand_on(HALF, o_last)
+        o_late = [tile([P, PIECE, PACK], BF16, "o_late%d" % c) for c in range(2)]
+        round_out(o_late[0][:], store(2, [acc2]))
+        nc.vector.tensor_copy(o_late[1][:], twin[:].rearrange("p t n -> p n t"))
+        store(3, last, nc.scalar)
+        for c in range(2):
+            hand_on(HALF + c * PIECE, o_late[c])
         for q in range(QUADS):
             queue = nc.sync if q % 2 else nc.scalar
             queue.dma_start(

@@ -259,11 +259,18 @@ def tile_picked_anc8_silu_po_kernel(
                 dst.rearrange("p (c i) t -> p c t i", i=4), o_f32[:].rearrange("p t (c i) -> p c t i", i=4)
             )
 
-        def hand_on(a, src, tag=None):
-            cols = slice(a, a + src.shape[1])
-            o_codes = tile([P, src.shape[1]], I32, "o_codes%d" % a, tag)
-            nc.vector.quantize_mx(o_codes[:].bitcast(FP8X4), o_scales[:, cols], src[:].rearrange("p n t -> p (n t)"))
-            nc.sync.dma_start(out_words[:, cols], o_codes[:])
+        def hand_on(half, pieces):
+            o_codes = tile([P, HALF], I32, "o_codes%d" % half)
+            a = 0
+            for src in pieces:
+                b = a + src.shape[1]
+                nc.vector.quantize_mx(
+                    o_codes[:, a:b].bitcast(FP8X4),
+                    o_scales[:, half * HALF + a : half * HALF + b],
+                    src[:].rearrange("p n t -> p (n t)"),
+                )
+                a = b
+            nc.sync.dma_start(out_words[:, half * HALF : (half + 1) * HALF], o_codes[:])
 
         nc.vector.tensor_copy(
             w2_sc[:].rearrange("p (t m) -> p m t", t=PACK), w2s_raw[:].rearrange("p (m t) -> p m t", t=PACK)
@@ -275,37 +282,42 @@ def tile_picked_anc8_silu_po_kernel(
         third(u, chain(1, 0, HALF, f1), 0, HALF)
         add_y(1)
         activate(z_first[:, :, EARLY:], u[:])
-        z_second = relay.tile([P, HALF, PACK], BF16, name="z_second", offset=2048, align_bytes=64)
+        z_second = relay.tile([P, HALF, PACK], BF16, name="z_second", offset=2560, align_bytes=64)
         z = [z_second[:, c * PIECE : (c + 1) * PIECE, :] for c in range(2)]
         activate(z_second[:, :, :EARLY], u_ps[1][:])
 
-        def late_piece(c, between):
-            a, b = HALF + c * PIECE, HALF + (c + 1) * PIECE
-            f1 = chain(0, a, b, [y_sb[1][t][:, c * PIECE : (c + 1) * PIECE] for t in range(2)])
-            f2 = chain(1, a, b, f1)
-            made = between()
-            u = relay.tile([P, PACK - EARLY, PIECE], F32, name="u%d" % c, offset=512 - 512 * c, align_bytes=64)
-            third(u, f2, a, b)
-            activate(z[c][:, :, EARLY:], u[:])
-            return made, u
+        f1 = chain(0, HALF, S, [y_sb[1][t][:] for t in range(2)])
 
-        zq, u = late_piece(0, lambda: quantise_z("z_first", z_first[:]))
+        def second(c, dst):
+            a = HALF + c * PIECE
+            for t in range(2):
+                look_up(dst[:, t, :], EARLY + t, 1, a, a + PIECE, f1[t][:, c * PIECE : (c + 1) * PIECE])
+            return [dst[:, t, :] for t in range(2)]
+
+        def finish(c, f2, u):
+            third(u, f2, HALF + c * PIECE, HALF + (c + 1) * PIECE)
+            activate(z[c][:, :, EARLY:], u[:])
+
+        f2 = second(0, tile([P, 2, PIECE], F32, "f2_0"))
+        zq = quantise_z("z_first", z_first[:])
+        finish(0, f2, relay.tile([P, 2, PIECE], F32, name="u0", offset=128, align_bytes=64))
         o = [store(c, [second_layer("acc%d" % c, zq, c * PIECE, range(PACK), "bank%d" % c)]) for c in range(2)]
-        zq, u = late_piece(1, lambda: quantise_z("z2", z[0]))
+        f2 = second(1, relay.tile([P, 2, PIECE], F32, name="f2_1", offset=1152, align_bytes=64))
+        finish(1, f2, tile([P, 2, PIECE], F32, "u1"))
+        zq = quantise_z("z2", z[0])
         acc2 = second_layer("acc2", zq, 0, range(PACK), "bank4")
         zq = quantise_z("z3", z[1])
         twin = second_layer("twin", zq, 0, range(PACK), "bank5")
         last = [second_layer("acc3_%d" % b, zq, 0, range(2 * b, 2 * b + 2), "bank%d" % (2 + b)) for b in range(2)]
-        o_first = tile([P, HALF, PACK], BF16, "o_first", "f1_0")
+        o_first = relay.tile([P, HALF, PACK], BF16, name="o_first", offset=0, align_bytes=64)
         for c in range(2):
             round_out(o_first[:, c * PIECE : (c + 1) * PIECE, :], o[c])
-        hand_on(0, o_first)
+        hand_on(0, [o_first])
         o_late = [tile([P, PIECE, PACK], BF16, "o_late%d" % c) for c in range(2)]
         round_out(o_late[0][:], store(2, [acc2]))
         nc.vector.tensor_copy(o_late[1][:], twin[:].rearrange("p t n -> p n t"))
         store(3, last, nc.scalar)
-        for c in range(2):
-            hand_on(HALF + c * PIECE, o_late[c])
+        hand_on(1, o_late)
         for q in range(QUADS):
             queue = nc.sync if q % 2 else nc.scalar
             queue.dma_start(

@@ -135,7 +135,7 @@ def tile_picked_anc8_silu_po_kernel(
         )
         quantise_w1(1, 0, round_w1(1, 0, EARLY), "x_all1")
 
-        u_ps = [ps.tile([P, EARLY, HALF], F32, name="u_ps%d" % h, tag="bank%d" % (6 + h)) for h in range(2)]
+        u_ps = [ps.tile([P, EARLY, HALF], F32, name="u_ps0", tag="bank6")]
 
         def turn_back(h, src, first):
             for c in range(2):
@@ -152,7 +152,8 @@ def tile_picked_anc8_silu_po_kernel(
         e_sb = tile([P, 2, 2, EARLY, P], F32, "e_sb", "w1_raw1")
         for h in range(2):
             nc.scalar.copy(e_sb[:, h], e_turned[h][:])
-            turn_back(h, e_sb[:, h], True)
+
+        turn_back(0, e_sb[:, 0], True)
 
         def first_layer(dst, t, g, h, start):
             half = slice(h * HALF, (h + 1) * HALF)
@@ -280,6 +281,8 @@ def tile_picked_anc8_silu_po_kernel(
         activate(z_first[:, :, :EARLY], u_ps[0][:])
         u = relay.tile([P, PACK - EARLY, HALF], F32, name="u_first", offset=1024, align_bytes=64)
         third(u, chain(1, 0, HALF, f1), 0, HALF)
+        u_ps.append(ps.tile([P, EARLY, HALF], F32, name="u_ps1", tag="bank1"))
+        turn_back(1, e_sb[:, 1], True)
         add_y(1)
         activate(z_first[:, :, EARLY:], u[:])
         z_second = relay.tile([P, HALF, PACK], BF16, name="z_second", offset=2560, align_bytes=64)
@@ -301,7 +304,7 @@ def tile_picked_anc8_silu_po_kernel(
         f2 = second(0, tile([P, 2, PIECE], F32, "f2_0"))
         zq = quantise_z("z_first", z_first[:])
         finish(0, f2, relay.tile([P, 2, PIECE], F32, name="u0", offset=128, align_bytes=64))
-        o = [store(c, [second_layer("acc%d" % c, zq, c * PIECE, range(PACK), "bank%d" % c)]) for c in range(2)]
+        o = [store(c, [second_layer("acc%d" % c, zq, c * PIECE, range(PACK), "bank%d" % (7 * c))]) for c in range(2)]
         f2 = second(1, relay.tile([P, 2, PIECE], F32, name="f2_1", offset=1152, align_bytes=64))
         finish(1, f2, tile([P, 2, PIECE], F32, "u1"))
         zq = quantise_z("z2", z[0])

@@ -1,7 +1,6 @@
 from contextlib import ExitStack
 
 import concourse.mybir as mybir
-from concourse.masks import make_identity
 
 K, T, S, N, H, U = 1024, 2048, 512, 512, 512, 512
 FLOPS = 2 * K * H * S + 2 * H * N * S
@@ -15,6 +14,7 @@ U8 = mybir.dt.uint8
 FP8X4 = mybir.dt.float8_e4m3fn_x4
 ADD = mybir.AluOpType.add
 SILU = mybir.ActivationFunctionType.Silu
+COPY = mybir.ActivationFunctionType.Copy
 
 P = 128
 PACK = 4
@@ -23,7 +23,6 @@ PIECE = 128
 PIECES = S // PIECE
 HALF = 256
 QUADS = 4
-EARLY = 2
 
 
 def tile_picked_anc8_silu_po_kernel(
@@ -38,289 +37,192 @@ def tile_picked_anc8_silu_po_kernel(
         def tile(shape, dtype, name, tag=None):
             return sb.tile(shape, dtype, name=name, tag=tag or name, align_bytes=64)
 
+        def placed(shape, dtype, name, offset):
+            return relay.tile(shape, dtype, name=name, offset=offset, align_bytes=64)
+
         lists = [tile([P, S // 16], U16, "up%d" % n) for n in range(3)]
         picked = tile([P, S // 16], U16, "picked")
-        table = [tile([P, 2 * U if t < EARLY else U], F32, "table%d" % t) for t in range(PACK)]
+        table = [tile([P, 2 * U], F32, "table%d" % t) for t in range(PACK)]
         w1_raw = [tile([P, PACK, H], F32, "w1_raw%d" % g) for g in range(PASSES)]
-        x_all = [tile([P, T], I32, "x_all%d" % g) for g in range(PASSES)]
+        x_all = [placed([P, T], I32, "x_all0", 0), tile([P, T], I32, "x_all1")]
         xs_all = tile([P, T], U8, "xs_all")
         w2_raw = tile([P, N], I32, "w2_raw")
         w2s_raw = tile([P, N], U8, "w2s_raw")
 
         nc.gpsimd.memset(xs_all[:].bitcast(I32), 0)
         nc.gpsimd.memset(w2s_raw[:].bitcast(I32), 0)
-        ident = tile([P, P], F32, "ident")
-        make_identity(nc, ident[:])
+
+        idle_in = tile([P, 1], F32, "idle_in")
+        idle_out = tile([P, 1], F32, "idle_out")
+        nc.vector.memset(idle_in[:], 0.0)
+        nc.scalar.activation(idle_out[:], idle_in[:], SILU)
 
         emb_rows = emb.rearrange("(p t) u -> t p u", t=PACK)
         w1_rows = w1.rearrange("(g p j) c -> g p j c", p=P, j=PACK)
+
+        def load_x(g):
+            nc.sync.dma_start(x_all[g][:], x_words[g].rearrange("p n t -> p (n t)").bitcast(I32))
+
         nc.sync.dma_start(table[0][:, :U], emb_rows[0])
         nc.sync.dma_start(lists[0][:], up1)
-        nc.sync.dma_start(table[1][:, :U], emb_rows[1])
         nc.sync.dma_start(lists[1][:], up2)
-        nc.sync.dma_start(w1_raw[0][:], w1_rows[0])
         nc.sync.dma_start(lists[2][:], up3)
+        for t in range(1, PACK):
+            nc.sync.dma_start(table[t][:, :U], emb_rows[t])
+        nc.sync.dma_start(w1_raw[0][:], w1_rows[0])
         nc.sync.dma_start(picked[:], offs)
         for q in range(QUADS):
             nc.sync.dma_start(
                 xs_all[32 * q : 32 * q + 4 * PASSES, :].bitcast(I32), x_scales[:, 4 * q : 4 * q + 4, :].bitcast(I32)
             )
+        load_x(0)
         nc.sync.dma_start(w1_raw[1][:], w1_rows[1])
-        for g in range(PASSES):
-            nc.sync.dma_start(x_all[g][:], x_words[g].rearrange("p n t -> p (n t)").bitcast(I32))
+        load_x(1)
         nc.sync.dma_start(w2_raw[:], w2_words[0].rearrange("p n t -> p (n t)").bitcast(I32))
         for q in range(QUADS):
             nc.sync.dma_start(
                 w2s_raw[32 * q : 32 * q + 4, :].bitcast(I32), w2_scales[0, 4 * q : 4 * q + 4, :].bitcast(I32)
             )
-        nc.sync.dma_start(table[2][:], emb_rows[2])
-        nc.sync.dma_start(table[3][:], emb_rows[3])
 
-        e1 = tile([P, EARLY, S], F32, "e1")
-        e2 = tile([P, EARLY, S], F32, "e2")
-        e3 = tile([P, EARLY, S], F32, "e3")
-        for t in range(EARLY):
-            nc.vector.tensor_copy(e1[:, t, :], table[t][:].indirect(lists[0][:]))
-        for t in range(EARLY):
-            nc.vector.tensor_tensor(e2[:, t, :], table[t][:].indirect(lists[1][:]), e1[:, t, :], ADD)
-        for t in range(EARLY):
-            nc.vector.tensor_tensor(e3[:, t, :], table[t][:].indirect(lists[2][:]), e2[:, t, :], ADD)
+        def fetch(dst, t, offsets):
+            nc.scalar.activation(dst, table[t][:].indirect(offsets), COPY)
 
-        e_turned = []
-        for h in range(2):
-            e_ps = ps.tile([P, 2, EARLY, P], F32, name="e_ps%d" % h, tag="bank%d" % (4 + h))
-            for c in range(2):
-                for t in range(EARLY):
-                    nc.tensor.transpose(
-                        e_ps[:, c, t, :], e3[:, t, h * HALF + c * P : h * HALF + (c + 1) * P], ident[:]
-                    )
-            e_turned.append(e_ps)
+        def fetch_add(dst, t, n, src):
+            nc.vector.tensor_tensor(dst, table[t][:].indirect(lists[n][:]), src, ADD)
 
-        def round_w1(g, a, b):
+        one = tile([P, PACK, S], F32, "one")
+        two = tile([P, PACK, S], F32, "two")
+        lone = tile([P, S], F32, "lone")
+        nc.vector.tensor_copy(lone[:], table[0][:].indirect(lists[1][:]))
+        for t in range(PACK):
+            fetch(one[:, t, :], t, lists[0][:])
+            fetch_add(two[:, t, :], t, 1 if t else 2, one[:, t, :])
+
+        def fetch_rest(h, tag):
+            rest = tile([P, PACK - 1, HALF], F32, "rest%d" % h, tag)
+            for t in range(1, PACK):
+                fetch(rest[:, t - 1, :], t, lists[2][:, h * HALF // 16 : (h + 1) * HALF // 16])
+            return rest
+
+        e = tile([P, PACK, S], F32, "e", "one")
+        nc.gpsimd.tensor_tensor(e[:, 0, :], two[:, 0, :], lone[:], ADD)
+
+        def sum_half(h, rest):
+            cols = slice(h * HALF, (h + 1) * HALF)
+            for t in range(1, PACK):
+                nc.gpsimd.tensor_tensor(e[:, t, cols], two[:, t, cols], rest[:, t - 1, :], ADD)
+
+        def round_w1(g, a, b, copy):
             w1_bf = tile([P, b - a, P, PACK], BF16, "w1_bf%d_%d" % (g, a))
-            nc.scalar.copy(
+            copy(
                 w1_bf[:].rearrange("p t m j -> p m j t"),
                 w1_raw[g][:].rearrange("p j (m t) -> p m j t", t=PACK)[:, :, :, a:b],
             )
             return w1_bf
 
         w1q = {}
-        w1_early = {}
 
-        def quantise_w1(g, a, w1_bf, tag):
+        def quantise_w1(g, a, w1_bf, codes):
             width = w1_bf.shape[1] * P
-            codes = tile([P, width], U32, "w1_codes%d_%d" % (g, a), tag)
             scales = tile([P, width], U8, "w1_scales%d_%d" % (g, a))
             nc.vector.quantize_mx(codes[:].bitcast(FP8X4), scales[:], w1_bf[:].rearrange("p t m j -> p (t m j)"))
-            if a == 0:
-                w1_early[g] = (codes[:, : EARLY * P], scales[:, : EARLY * P])
             for t in range(w1_bf.shape[1]):
                 w1q[g, a + t] = (codes[:, t * P : (t + 1) * P], scales[:, t * P : (t + 1) * P])
 
         xs = tile([P, S], U8, "xs")
         xg0 = tile([P, S], U32, "xg0")
         xg1 = [tile([P, HALF], U32, "xg1_%d" % h) for h in range(2)]
-        quantise_w1(0, 0, round_w1(0, 0, PACK), None)
         nc.vector.tensor_copy(xs[:], xs_all[:].indirect(picked[:]))
-        quantise_w1(1, EARLY, round_w1(1, EARLY, PACK), None)
+        sum_half(0, fetch_rest(0, None))
         nc.vector.tensor_copy(xg0[:], x_all[0][:].bitcast(U32).indirect(picked[:]))
+        quantise_w1(0, 0, round_w1(0, 0, PACK, nc.scalar.copy), placed([P, H], U32, "w1_codes0", 0))
+        late = round_w1(1, 2, PACK, nc.vector.tensor_copy)
+        quantise_w1(1, 0, round_w1(1, 0, 2, nc.scalar.copy), tile([P, H // 2], U32, "w1_codes1_0"))
+        quantise_w1(1, 2, late, tile([P, H // 2], U32, "w1_codes1_2"))
         for h in range(2):
             nc.vector.tensor_copy(
                 xg1[h][:], x_all[1][:].bitcast(U32).indirect(picked[:, h * HALF // 16 : (h + 1) * HALF // 16])
             )
-        w2_codes = tile([P, N], I32, "w2_codes")
+        sum_half(1, fetch_rest(1, "w1_raw1"))
+        w2_codes = tile([P, N], U32, "w2_codes")
         w2_sc = tile([P, N], U8, "w2_sc")
-        nc.vector.tensor_copy(
-            w2_codes[:].rearrange("p (t m) -> p m t", t=PACK), w2_raw[:].rearrange("p (m t) -> p m t", t=PACK)
+        nc.scalar.copy(
+            w2_codes[:].rearrange("p (t m) -> p m t", t=PACK),
+            w2_raw[:].bitcast(U32).rearrange("p (m t) -> p m t", t=PACK),
         )
-        quantise_w1(1, 0, round_w1(1, 0, EARLY), "x_all1")
+        nc.vector.tensor_copy(
+            w2_sc[:].rearrange("p (t m) -> p m t", t=PACK), w2s_raw[:].rearrange("p (m t) -> p m t", t=PACK)
+        )
 
-        u_ps = [ps.tile([P, EARLY, HALF], F32, name="u_ps0", tag="bank6")]
-
-        def turn_back(h, src, first):
-            for c in range(2):
-                for t in range(EARLY):
-                    nc.tensor.matmul(
-                        u_ps[h][:, t, c * P : (c + 1) * P],
-                        lhsT=src[:, c, t, :],
-                        rhs=ident[:],
-                        is_transpose=True,
-                        start=first and c == 0 and t == 0,
-                        stop=not first and c == 1 and t == EARLY - 1,
-                    )
-
-        e_sb = tile([P, 2, 2, EARLY, P], F32, "e_sb", "w1_raw1")
-        for h in range(2):
-            nc.scalar.copy(e_sb[:, h], e_turned[h][:])
-
-        turn_back(0, e_sb[:, 0], True)
-
-        def first_layer(dst, t, g, h, start):
-            half = slice(h * HALF, (h + 1) * HALF)
-            nc.tensor.matmul_mx(
-                dst,
-                lhsT=w1q[g, t][0].bitcast(FP8X4),
-                lhsT_scale=w1q[g, t][1],
-                rhs=(xg1[h][:] if g else xg0[:, half]).bitcast(FP8X4),
-                rhs_scale=xs[4 * g : P, half],
-                start=start,
-                stop=not start,
-            )
-
-        y_late = [
-            [ps.tile([P, HALF], F32, name="y%d_%d" % (h, t), tag="bank%d" % (2 * h + t)) for t in range(2)]
-            for h in range(2)
-        ]
-        y_early = [ps.tile([P, 2, EARLY, P], F32, name="ye%d" % h, tag="bank%d" % (4 + h)) for h in range(2)]
+        y = [ps.tile([P, PACK, PIECE], F32, name="y%d" % c, tag="bank%d" % c) for c in range(PIECES)]
         for g in range(PASSES):
-            for t in range(2):
-                first_layer(y_late[0][t][:], EARLY + t, g, 0, g == 0)
-        for t in range(2):
-            for g in reversed(range(PASSES)):
-                first_layer(y_late[1][t][:], EARLY + t, g, 1, g == PASSES - 1)
-        for h in range(2):
-            for c in range(2):
-                cols = slice(h * HALF + c * P, h * HALF + (c + 1) * P)
-                for g in reversed(range(PASSES)):
+            for c in range(PIECES):
+                cols = slice(c * PIECE, (c + 1) * PIECE)
+                for t in range(PACK):
                     nc.tensor.matmul_mx(
-                        y_early[h][:, c, :, :].rearrange("p t m -> p (t m)"),
-                        lhsT=(xg1[h][:, c * P : (c + 1) * P] if g else xg0[:, cols]).bitcast(FP8X4),
-                        lhsT_scale=xs[4 * g : P, cols],
-                        rhs=w1_early[g][0].bitcast(FP8X4),
-                        rhs_scale=w1_early[g][1],
-                        start=g == PASSES - 1,
-                        stop=g == 0,
+                        y[c][:, t, :],
+                        lhsT=w1q[g, t][0].bitcast(FP8X4),
+                        lhsT_scale=w1q[g, t][1],
+                        rhs=(xg1[c // 2][:, c % 2 * PIECE : (c % 2 + 1) * PIECE] if g else xg0[:, cols]).bitcast(FP8X4),
+                        rhs_scale=xs[4 * g : P, cols],
+                        start=g == 0 and t == 0,
+                        stop=g == PASSES - 1 and t == PACK - 1,
                     )
-
-        y_sb = [[tile([P, HALF], F32, "y_sb%d_%d" % (a, t)) for t in range(PACK - EARLY)] for a in range(2)]
-        for h in range(2):
-            for t in range(2):
-                nc.scalar.copy(y_sb[h][t][:], y_late[h][t][:])
 
         out_rows = out_0.rearrange("(p t) j -> p t j", t=PACK)
         out_words = out_1[0].rearrange("p n t -> p (n t)").bitcast(I32)
         o_scales = tile([P, S], U8, "o_scales")
 
-        def look_up(dst, t, n, a, b, src):
-            nc.vector.tensor_tensor(dst, table[t][:].indirect(lists[n][:, a // 16 : b // 16]), src, ADD)
+        def woven(dst):
+            return dst.rearrange("p (c i) t -> p c t i", i=4)
 
-        z_first = tile([P, HALF, PACK], BF16, "z_first")
+        def planar(src):
+            return src.rearrange("p t (c i) -> p c t i", i=4)
 
-        def chain(n, a, b, src):
-            dst = [tile([P, b - a], F32, "f%d_%d_%d" % (n, a, t), "f%d_%d" % (n, t)) for t in range(2)]
-            for t in range(2):
-                look_up(dst[t][:], EARLY + t, n, a, b, src[t])
-            return [d[:] for d in dst]
+        def hidden(c):
+            u = tile([P, PACK, PIECE], F32, "u%d" % c)
+            nc.vector.tensor_tensor(u[:], y[c][:], e[:, :, c * PIECE : (c + 1) * PIECE], ADD)
+            z_bf = tile([P, PIECE, PACK], BF16, "z%d" % c)
+            nc.scalar.activation(woven(z_bf[:]), planar(u[:]), SILU)
+            return z_bf
 
-        def third(u, f2, a, b):
-            for t in range(2):
-                look_up(u[:, t, :], EARLY + t, 2, a, b, f2[t])
-
-        def activate(dst, src):
-            nc.scalar.activation(
-                dst.rearrange("p (c i) t -> p c t i", i=4), src.rearrange("p t (c i) -> p c t i", i=4), SILU
-            )
-
-        def add_y(h):
-            y_turned = tile([P, 2, EARLY, P], F32, "y_turned%d" % h)
-            nc.scalar.copy(y_turned[:], y_early[h][:])
-            turn_back(h, y_turned, False)
-
-        def quantise_z(name, z_bf):
-            z_codes = tile([P, z_bf.shape[1]], U32, name + "_codes")
-            z_scales = tile([P, z_bf.shape[1]], U8, name + "_scales")
-            nc.vector.quantize_mx(z_codes[:].bitcast(FP8X4), z_scales[:], z_bf.rearrange("p n t -> p (n t)"))
-            return z_codes, z_scales
-
-        def second_layer(name, zq, a, planes, bank):
-            acc = ps.tile([P, len(planes), PIECE], F32, name=name, tag=bank)
-            for n, t in enumerate(planes):
+        def second_layer(c, z_bf):
+            z_codes = tile([P, PIECE], U32, "z_codes%d" % c)
+            z_scales = tile([P, PIECE], U8, "z_scales%d" % c)
+            nc.vector.quantize_mx(z_codes[:].bitcast(FP8X4), z_scales[:], z_bf[:].rearrange("p n t -> p (n t)"))
+            acc = ps.tile([P, PACK, PIECE], F32, name="acc%d" % c, tag="bank%d" % (PIECES + c))
+            for t in range(PACK):
                 cols = slice(t * P, (t + 1) * P)
                 nc.tensor.matmul_mx(
-                    acc[:, n, :],
+                    acc[:, t, :],
                     lhsT=w2_codes[:, cols].bitcast(FP8X4),
                     lhsT_scale=w2_sc[:, cols],
-                    rhs=zq[0][:, a : a + PIECE].bitcast(FP8X4),
-                    rhs_scale=zq[1][:, a : a + PIECE],
+                    rhs=z_codes[:].bitcast(FP8X4),
+                    rhs_scale=z_scales[:],
                     start=True,
                     stop=True,
                 )
             return acc
 
-        def store(c, accs, queue=nc.sync):
+        def store(c, acc, o_bf):
             o_f32 = tile([P, PACK, PIECE], F32, "o_f32%d" % c)
-            per = PACK // len(accs)
-            for b, acc in enumerate(accs):
-                nc.scalar.copy(o_f32[:, b * per : (b + 1) * per, :], acc[:])
-            queue.dma_start(out_rows[:, :, c * PIECE : (c + 1) * PIECE], o_f32[:])
-            return o_f32
+            nc.scalar.copy(o_f32[:], acc[:])
+            nc.sync.dma_start(out_rows[:, :, c * PIECE : (c + 1) * PIECE], o_f32[:])
+            nc.vector.tensor_copy(woven(o_bf), planar(o_f32[:]))
 
-        def round_out(dst, o_f32):
-            nc.vector.tensor_copy(
-                dst.rearrange("p (c i) t -> p c t i", i=4), o_f32[:].rearrange("p t (c i) -> p c t i", i=4)
-            )
-
-        def hand_on(half, pieces):
+        def hand_on(half, o_bf):
             o_codes = tile([P, HALF], I32, "o_codes%d" % half)
-            a = 0
-            for src in pieces:
-                b = a + src.shape[1]
-                nc.vector.quantize_mx(
-                    o_codes[:, a:b].bitcast(FP8X4),
-                    o_scales[:, half * HALF + a : half * HALF + b],
-                    src[:].rearrange("p n t -> p (n t)"),
-                )
-                a = b
-            nc.sync.dma_start(out_words[:, half * HALF : (half + 1) * HALF], o_codes[:])
+            cols = slice(half * HALF, (half + 1) * HALF)
+            nc.vector.quantize_mx(o_codes[:].bitcast(FP8X4), o_scales[:, cols], o_bf[:].rearrange("p n t -> p (n t)"))
+            nc.sync.dma_start(out_words[:, cols], o_codes[:])
 
-        nc.vector.tensor_copy(
-            w2_sc[:].rearrange("p (t m) -> p m t", t=PACK), w2s_raw[:].rearrange("p (m t) -> p m t", t=PACK)
-        )
-        f1 = chain(0, 0, HALF, [y_sb[0][t][:] for t in range(2)])
-        add_y(0)
-        activate(z_first[:, :, :EARLY], u_ps[0][:])
-        u = relay.tile([P, PACK - EARLY, HALF], F32, name="u_first", offset=1024, align_bytes=64)
-        third(u, chain(1, 0, HALF, f1), 0, HALF)
-        u_ps.append(ps.tile([P, EARLY, HALF], F32, name="u_ps1", tag="bank1"))
-        turn_back(1, e_sb[:, 1], True)
-        add_y(1)
-        activate(z_first[:, :, EARLY:], u[:])
-        z_second = relay.tile([P, HALF, PACK], BF16, name="z_second", offset=2560, align_bytes=64)
-        z = [z_second[:, c * PIECE : (c + 1) * PIECE, :] for c in range(2)]
-        activate(z_second[:, :, :EARLY], u_ps[1][:])
-
-        f1 = chain(0, HALF, S, [y_sb[1][t][:] for t in range(2)])
-
-        def second(c, dst):
-            a = HALF + c * PIECE
-            for t in range(2):
-                look_up(dst[:, t, :], EARLY + t, 1, a, a + PIECE, f1[t][:, c * PIECE : (c + 1) * PIECE])
-            return [dst[:, t, :] for t in range(2)]
-
-        def finish(c, f2, u):
-            third(u, f2, HALF + c * PIECE, HALF + (c + 1) * PIECE)
-            activate(z[c][:, :, EARLY:], u[:])
-
-        f2 = second(0, tile([P, 2, PIECE], F32, "f2_0"))
-        zq = quantise_z("z_first", z_first[:])
-        finish(0, f2, relay.tile([P, 2, PIECE], F32, name="u0", offset=128, align_bytes=64))
-        o = [store(c, [second_layer("acc%d" % c, zq, c * PIECE, range(PACK), "bank%d" % (7 * c))]) for c in range(2)]
-        f2 = second(1, relay.tile([P, 2, PIECE], F32, name="f2_1", offset=1152, align_bytes=64))
-        finish(1, f2, tile([P, 2, PIECE], F32, "u1"))
-        zq = quantise_z("z2", z[0])
-        acc2 = second_layer("acc2", zq, 0, range(PACK), "bank4")
-        zq = quantise_z("z3", z[1])
-        twin = second_layer("twin", zq, 0, range(PACK), "bank5")
-        last = [second_layer("acc3_%d" % b, zq, 0, range(2 * b, 2 * b + 2), "bank%d" % (2 + b)) for b in range(2)]
-        o_first = relay.tile([P, HALF, PACK], BF16, name="o_first", offset=0, align_bytes=64)
-        for c in range(2):
-            round_out(o_first[:, c * PIECE : (c + 1) * PIECE, :], o[c])
-        hand_on(0, [o_first])
-        o_late = [tile([P, PIECE, PACK], BF16, "o_late%d" % c) for c in range(2)]
-        round_out(o_late[0][:], store(2, [acc2]))
-        nc.vector.tensor_copy(o_late[1][:], twin[:].rearrange("p t n -> p n t"))
-        store(3, last, nc.scalar)
-        hand_on(1, o_late)
+        z = [hidden(c) for c in range(PIECES)]
+        accs = [second_layer(c, z[c]) for c in range(PIECES)]
+        for half in range(2):
+            o_bf = tile([P, HALF, PACK], BF16, "o_bf%d" % half)
+            for c in range(2):
+                store(2 * half + c, accs[2 * half + c], o_bf[:, c * PIECE : (c + 1) * PIECE, :])
+            hand_on(half, o_bf)
         for q in range(QUADS):
             queue = nc.sync if q % 2 else nc.scalar
             queue.dma_start(

@@ -77,12 +77,12 @@ def tile_picked_anc8_silu_po_kernel(
             )
         load_x(0)
         nc.sync.dma_start(w1_raw[1][:], w1_rows[1])
-        load_x(1)
-        nc.sync.dma_start(w2_raw[:], w2_words[0].rearrange("p n t -> p (n t)").bitcast(I32))
         for q in range(QUADS):
             nc.sync.dma_start(
                 w2s_raw[32 * q : 32 * q + 4, :].bitcast(I32), w2_scales[0, 4 * q : 4 * q + 4, :].bitcast(I32)
             )
+        load_x(1)
+        nc.sync.dma_start(w2_raw[:], w2_words[0].rearrange("p n t -> p (n t)").bitcast(I32))
 
         def fetch(dst, t, offsets):
             nc.scalar.activation(dst, table[t][:].indirect(offsets), COPY)
@@ -92,28 +92,18 @@ def tile_picked_anc8_silu_po_kernel(
 
         one = tile([P, PACK, S], F32, "one")
         two = tile([P, PACK, S], F32, "two")
-        lone = tile([P, S], F32, "lone")
-        nc.vector.tensor_copy(lone[:], table[0][:].indirect(lists[1][:]))
+        rest_first = tile([P, PACK, S], F32, "rest_first")
+        nc.vector.tensor_copy(rest_first[:, 0, :], table[0][:].indirect(lists[1][:]))
         for t in range(PACK):
             fetch(one[:, t, :], t, lists[0][:])
             fetch_add(two[:, t, :], t, 1 if t else 2, one[:, t, :])
+        for t in range(1, PACK):
+            fetch(rest_first[:, t, :HALF], t, lists[2][:, : HALF // 16])
+        e = [tile([P, PACK, HALF], F32, "e0", "one")]
+        nc.gpsimd.tensor_tensor(e[0][:], two[:, :, :HALF], rest_first[:, :, :HALF], ADD)
 
-        def fetch_rest(h, tag):
-            rest = tile([P, PACK - 1, HALF], F32, "rest%d" % h, tag)
-            for t in range(1, PACK):
-                fetch(rest[:, t - 1, :], t, lists[2][:, h * HALF // 16 : (h + 1) * HALF // 16])
-            return rest
-
-        e = tile([P, PACK, S], F32, "e", "one")
-        nc.gpsimd.tensor_tensor(e[:, 0, :], two[:, 0, :], lone[:], ADD)
-
-        def sum_half(h, rest):
-            cols = slice(h * HALF, (h + 1) * HALF)
-            for t in range(1, PACK):
-                nc.gpsimd.tensor_tensor(e[:, t, cols], two[:, t, cols], rest[:, t - 1, :], ADD)
-
-        def round_w1(g, a, b, copy):
-            w1_bf = tile([P, b - a, P, PACK], BF16, "w1_bf%d_%d" % (g, a))
+        def round_w1(g, a, b, copy, tag=None):
+            w1_bf = tile([P, b - a, P, PACK], BF16, "w1_bf%d_%d" % (g, a), tag)
             copy(
                 w1_bf[:].rearrange("p t m j -> p m j t"),
                 w1_raw[g][:].rearrange("p j (m t) -> p m j t", t=PACK)[:, :, :, a:b],
@@ -133,17 +123,22 @@ def tile_picked_anc8_silu_po_kernel(
         xg0 = tile([P, S], U32, "xg0")
         xg1 = [tile([P, HALF], U32, "xg1_%d" % h) for h in range(2)]
         nc.vector.tensor_copy(xs[:], xs_all[:].indirect(picked[:]))
-        sum_half(0, fetch_rest(0, None))
         nc.vector.tensor_copy(xg0[:], x_all[0][:].bitcast(U32).indirect(picked[:]))
         quantise_w1(0, 0, round_w1(0, 0, PACK, nc.scalar.copy), placed([P, H], U32, "w1_codes0", 0))
-        late = round_w1(1, 2, PACK, nc.vector.tensor_copy)
+        late = round_w1(1, 2, PACK, nc.vector.tensor_copy, "e1")
         quantise_w1(1, 0, round_w1(1, 0, 2, nc.scalar.copy), tile([P, H // 2], U32, "w1_codes1_0"))
         quantise_w1(1, 2, late, tile([P, H // 2], U32, "w1_codes1_2"))
         for h in range(2):
             nc.vector.tensor_copy(
                 xg1[h][:], x_all[1][:].bitcast(U32).indirect(picked[:, h * HALF // 16 : (h + 1) * HALF // 16])
             )
-        sum_half(1, fetch_rest(1, "w1_raw1"))
+        rest_second = tile([P, PACK - 1, HALF], F32, "rest_second", "w1_raw1")
+        for t in range(1, PACK):
+            fetch(rest_second[:, t - 1, :], t, lists[2][:, HALF // 16 :])
+        e.append(tile([P, PACK, HALF], F32, "e1"))
+        nc.gpsimd.tensor_tensor(e[1][:, 0, :], two[:, 0, HALF:], rest_first[:, 0, HALF:], ADD)
+        nc.gpsimd.tensor_tensor(e[1][:, 1:3, :], two[:, 1:3, HALF:], rest_second[:, :2, :], ADD)
+        nc.gpsimd.tensor_tensor(e[1][:, 3, :], two[:, 3, HALF:], rest_second[:, 2, :], ADD)
         w2_codes = tile([P, N], U32, "w2_codes")
         w2_sc = tile([P, N], U8, "w2_sc")
         nc.scalar.copy(
@@ -181,7 +176,7 @@ def tile_picked_anc8_silu_po_kernel(
 
         def hidden(c):
             u = tile([P, PACK, PIECE], F32, "u%d" % c)
-            nc.vector.tensor_tensor(u[:], y[c][:], e[:, :, c * PIECE : (c + 1) * PIECE], ADD)
+            nc.vector.tensor_tensor(u[:], y[c][:], e[c // 2][:, :, c % 2 * PIECE : (c % 2 + 1) * PIECE], ADD)
             z_bf = tile([P, PIECE, PACK], BF16, "z%d" % c)
             nc.scalar.activation(woven(z_bf[:]), planar(u[:]), SILU)
             return z_bf

@@ -1,6 +1,7 @@
 from contextlib import ExitStack
 
 import concourse.mybir as mybir
+from concourse.masks import make_identity
 
 K, T, S, N, H, U = 1024, 2048, 512, 512, 512, 512
 FLOPS = 2 * K * H * S + 2 * H * N * S
@@ -13,6 +14,7 @@ U16 = mybir.dt.uint16
 U8 = mybir.dt.uint8
 FP8X4 = mybir.dt.float8_e4m3fn_x4
 ADD = mybir.AluOpType.add
+MULT = mybir.AluOpType.mult
 SILU = mybir.ActivationFunctionType.Silu
 COPY = mybir.ActivationFunctionType.Copy
 
@@ -23,6 +25,7 @@ PIECE = 128
 PIECES = S // PIECE
 HALF = 256
 QUADS = 4
+LISTS = 3
 
 
 def tile_picked_anc8_silu_po_kernel(
@@ -31,26 +34,24 @@ def tile_picked_anc8_silu_po_kernel(
     nc = tc.nc
     with ExitStack() as ctx:
         sb = ctx.enter_context(tc.tile_pool(name="sb", bufs=1))
-        relay = ctx.enter_context(tc.tile_pool(name="relay", bufs=1))
         ps = ctx.enter_context(tc.psum_pool(name="ps", bufs=1))
 
         def tile(shape, dtype, name, tag=None):
             return sb.tile(shape, dtype, name=name, tag=tag or name, align_bytes=64)
 
-        def placed(shape, dtype, name, offset):
-            return relay.tile(shape, dtype, name=name, offset=offset, align_bytes=64)
-
-        lists = [tile([P, S // 16], U16, "up%d" % n) for n in range(3)]
+        lists = [tile([P, S // 16], U16, "up%d" % n) for n in range(LISTS)]
         picked = tile([P, S // 16], U16, "picked")
         table = [tile([P, 2 * U], F32, "table%d" % t) for t in range(PACK)]
         w1_raw = [tile([P, PACK, H], F32, "w1_raw%d" % g) for g in range(PASSES)]
-        x_all = [placed([P, T], I32, "x_all0", 0), tile([P, T], I32, "x_all1")]
+        x_all = [tile([P, T], I32, "x_all%d" % g) for g in range(PASSES)]
         xs_all = tile([P, T], U8, "xs_all")
         w2_raw = tile([P, N], I32, "w2_raw")
         w2s_raw = tile([P, N], U8, "w2s_raw")
+        ident = tile([P, P], F32, "ident")
 
         nc.gpsimd.memset(xs_all[:].bitcast(I32), 0)
         nc.gpsimd.memset(w2s_raw[:].bitcast(I32), 0)
+        make_identity(nc, ident[:])
 
         idle_in = tile([P, 1], F32, "idle_in")
         idle_out = tile([P, 1], F32, "idle_out")
@@ -67,16 +68,17 @@ def tile_picked_anc8_silu_po_kernel(
         nc.sync.dma_start(lists[0][:], up1)
         nc.sync.dma_start(lists[1][:], up2)
         nc.sync.dma_start(lists[2][:], up3)
-        for t in range(1, PACK):
-            nc.sync.dma_start(table[t][:, :U], emb_rows[t])
+        nc.sync.dma_start(table[1][:, :U], emb_rows[1])
         nc.sync.dma_start(w1_raw[0][:], w1_rows[0])
+        nc.sync.dma_start(table[2][:, :U], emb_rows[2])
+        nc.sync.dma_start(table[3][:, :U], emb_rows[3])
         nc.sync.dma_start(picked[:], offs)
         for q in range(QUADS):
             nc.sync.dma_start(
                 xs_all[32 * q : 32 * q + 4 * PASSES, :].bitcast(I32), x_scales[:, 4 * q : 4 * q + 4, :].bitcast(I32)
             )
-        load_x(0)
         nc.sync.dma_start(w1_raw[1][:], w1_rows[1])
+        load_x(0)
         for q in range(QUADS):
             nc.sync.dma_start(
                 w2s_raw[32 * q : 32 * q + 4, :].bitcast(I32), w2_scales[0, 4 * q : 4 * q + 4, :].bitcast(I32)
@@ -84,85 +86,74 @@ def tile_picked_anc8_silu_po_kernel(
         load_x(1)
         nc.sync.dma_start(w2_raw[:], w2_words[0].rearrange("p n t -> p (n t)").bitcast(I32))
 
-        def fetch(dst, t, offsets):
-            nc.scalar.activation(dst, table[t][:].indirect(offsets), COPY)
-
-        def fetch_add(dst, t, n, src):
-            nc.vector.tensor_tensor(dst, table[t][:].indirect(lists[n][:]), src, ADD)
-
-        one = tile([P, PACK, S], F32, "one")
-        two = tile([P, PACK, S], F32, "two")
-        rest_first = tile([P, PACK, S], F32, "rest_first")
-        nc.vector.tensor_copy(rest_first[:, 0, :], table[0][:].indirect(lists[1][:]))
+        e_turned = tile([P, PACK, PIECES, P], F32, "e_turned")
         for t in range(PACK):
-            fetch(one[:, t, :], t, lists[0][:])
-            fetch_add(two[:, t, :], t, 1 if t else 2, one[:, t, :])
-        for t in range(1, PACK):
-            fetch(rest_first[:, t, :HALF], t, lists[2][:, : HALF // 16])
-        e = [tile([P, PACK, HALF], F32, "e0", "one")]
-        nc.gpsimd.tensor_tensor(e[0][:], two[:, :, :HALF], rest_first[:, :, :HALF], ADD)
+            bank = ps.tile([P, PIECES, P], F32, name="e_sum%d" % t, tag="bank%d" % t)
+            for n in range(LISTS):
+                got = tile([P, S], F32, "got%d_%d" % (t, n))
+                step = LISTS * t + n
+                if step % 2 and step < 8:
+                    nc.vector.tensor_copy(got[:], table[t][:].indirect(lists[n][:]))
+                else:
+                    nc.scalar.activation(got[:], table[t][:].indirect(lists[n][:]), COPY)
+                for c in range(PIECES):
+                    nc.tensor.matmul(
+                        bank[:, c, :],
+                        lhsT=got[:, c * PIECE : (c + 1) * PIECE],
+                        rhs=ident[:],
+                        is_transpose=True,
+                        start=n == 0 and c == 0,
+                        stop=n == LISTS - 1 and c == PIECES - 1,
+                    )
+            if t < 2:
+                nc.vector.tensor_copy(e_turned[:, t, :, :], bank[:])
+            else:
+                nc.scalar.copy(e_turned[:, t, :, :], bank[:])
 
-        def round_w1(g, a, b, copy, tag=None):
-            w1_bf = tile([P, b - a, P, PACK], BF16, "w1_bf%d_%d" % (g, a), tag)
-            copy(
-                w1_bf[:].rearrange("p t m j -> p m j t"),
-                w1_raw[g][:].rearrange("p j (m t) -> p m j t", t=PACK)[:, :, :, a:b],
-            )
-            return w1_bf
+        w1_codes = [tile([P, H], U32, "w1_codes0"), None]
+        w1_scales = [tile([P, H], U8, "w1_scales%d" % g) for g in range(PASSES)]
 
-        w1q = {}
+        def quantise_w1(g):
+            w1_bf = tile([P, H, PACK], BF16, "w1_bf%d" % g, "w1_bf")
+            nc.gpsimd.tensor_scalar(w1_bf[:], w1_raw[g][:].rearrange("p j c -> p c j"), 1.0, 0.0, MULT, ADD)
+            nc.vector.quantize_mx(w1_codes[g][:].bitcast(FP8X4), w1_scales[g][:], w1_bf[:].rearrange("p c j -> p (c j)"))
 
-        def quantise_w1(g, a, w1_bf, codes):
-            width = w1_bf.shape[1] * P
-            scales = tile([P, width], U8, "w1_scales%d_%d" % (g, a))
-            nc.vector.quantize_mx(codes[:].bitcast(FP8X4), scales[:], w1_bf[:].rearrange("p t m j -> p (t m j)"))
-            for t in range(w1_bf.shape[1]):
-                w1q[g, a + t] = (codes[:, t * P : (t + 1) * P], scales[:, t * P : (t + 1) * P])
+        quantise_w1(0)
 
         xs = tile([P, S], U8, "xs")
         xg0 = tile([P, S], U32, "xg0")
         xg1 = [tile([P, HALF], U32, "xg1_%d" % h) for h in range(2)]
         nc.vector.tensor_copy(xs[:], xs_all[:].indirect(picked[:]))
         nc.vector.tensor_copy(xg0[:], x_all[0][:].bitcast(U32).indirect(picked[:]))
-        quantise_w1(0, 0, round_w1(0, 0, PACK, nc.scalar.copy), placed([P, H], U32, "w1_codes0", 0))
-        late = round_w1(1, 2, PACK, nc.vector.tensor_copy, "e1")
-        quantise_w1(1, 0, round_w1(1, 0, 2, nc.scalar.copy), tile([P, H // 2], U32, "w1_codes1_0"))
-        quantise_w1(1, 2, late, tile([P, H // 2], U32, "w1_codes1_2"))
+        w1_codes[1] = tile([P, H], U32, "w1_codes1", "x_all0")
+        quantise_w1(1)
+        w2_codes = tile([P, N], U32, "w2_codes")
+        w2_sc = tile([P, N], U8, "w2_sc")
+        nc.vector.tensor_copy(
+            w2_sc[:].rearrange("p (t m) -> p m t", t=PACK), w2s_raw[:].rearrange("p (m t) -> p m t", t=PACK)
+        )
         for h in range(2):
             nc.vector.tensor_copy(
                 xg1[h][:], x_all[1][:].bitcast(U32).indirect(picked[:, h * HALF // 16 : (h + 1) * HALF // 16])
             )
-        rest_second = tile([P, PACK - 1, HALF], F32, "rest_second", "w1_raw1")
-        for t in range(1, PACK):
-            fetch(rest_second[:, t - 1, :], t, lists[2][:, HALF // 16 :])
-        e.append(tile([P, PACK, HALF], F32, "e1"))
-        nc.gpsimd.tensor_tensor(e[1][:, 0, :], two[:, 0, HALF:], rest_first[:, 0, HALF:], ADD)
-        nc.gpsimd.tensor_tensor(e[1][:, 1:3, :], two[:, 1:3, HALF:], rest_second[:, :2, :], ADD)
-        nc.gpsimd.tensor_tensor(e[1][:, 3, :], two[:, 3, HALF:], rest_second[:, 2, :], ADD)
-        w2_codes = tile([P, N], U32, "w2_codes")
-        w2_sc = tile([P, N], U8, "w2_sc")
         nc.scalar.copy(
             w2_codes[:].rearrange("p (t m) -> p m t", t=PACK),
             w2_raw[:].bitcast(U32).rearrange("p (m t) -> p m t", t=PACK),
         )
-        nc.vector.tensor_copy(
-            w2_sc[:].rearrange("p (t m) -> p m t", t=PACK), w2s_raw[:].rearrange("p (m t) -> p m t", t=PACK)
-        )
 
-        y = [ps.tile([P, PACK, PIECE], F32, name="y%d" % c, tag="bank%d" % c) for c in range(PIECES)]
+        y = [ps.tile([P, H], F32, name="y%d" % c, tag="bank%d" % (PACK + c)) for c in range(PIECES)]
         for g in range(PASSES):
             for c in range(PIECES):
                 cols = slice(c * PIECE, (c + 1) * PIECE)
-                for t in range(PACK):
-                    nc.tensor.matmul_mx(
-                        y[c][:, t, :],
-                        lhsT=w1q[g, t][0].bitcast(FP8X4),
-                        lhsT_scale=w1q[g, t][1],
-                        rhs=(xg1[c // 2][:, c % 2 * PIECE : (c % 2 + 1) * PIECE] if g else xg0[:, cols]).bitcast(FP8X4),
-                        rhs_scale=xs[4 * g : P, cols],
-                        start=g == 0 and t == 0,
-                        stop=g == PASSES - 1 and t == PACK - 1,
-                    )
+                nc.tensor.matmul_mx(
+                    y[c][:],
+                    lhsT=(xg1[c // 2][:, c % 2 * PIECE : (c % 2 + 1) * PIECE] if g else xg0[:, cols]).bitcast(FP8X4),
+                    lhsT_scale=xs[4 * g : P, cols],
+                    rhs=w1_codes[g][:].bitcast(FP8X4),
+                    rhs_scale=w1_scales[g][:],
+                    start=g == 0,
+                    stop=g == PASSES - 1,
+                )
 
         out_rows = out_0.rearrange("(p t) j -> p t j", t=PACK)
         out_words = out_1[0].rearrange("p n t -> p (n t)").bitcast(I32)
@@ -174,9 +165,23 @@ def tile_picked_anc8_silu_po_kernel(
         def planar(src):
             return src.rearrange("p t (c i) -> p c t i", i=4)
 
+        def turn(dst, src, first, last):
+            for t in range(PACK):
+                nc.tensor.matmul(
+                    dst[:, t, :],
+                    lhsT=src[:, t, :],
+                    rhs=ident[:],
+                    is_transpose=True,
+                    start=first and t == 0,
+                    stop=last and t == PACK - 1,
+                )
+
         def hidden(c):
-            u = tile([P, PACK, PIECE], F32, "u%d" % c)
-            nc.vector.tensor_tensor(u[:], y[c][:], e[c // 2][:, :, c % 2 * PIECE : (c % 2 + 1) * PIECE], ADD)
+            u = ps.tile([P, PACK, PIECE], F32, name="u%d" % c, tag="bank%d" % c)
+            y_dealt = y[c][:].rearrange("j (p t) -> j t p", t=PACK)
+            turned = tile([P, PACK, P], F32, "turned%d" % c)
+            nc.vector.tensor_tensor(turned[:], y_dealt, e_turned[:, :, c, :], ADD)
+            turn(u, turned, True, True)
             z_bf = tile([P, PIECE, PACK], BF16, "z%d" % c)
             nc.scalar.activation(woven(z_bf[:]), planar(u[:]), SILU)
             return z_bf
@@ -185,7 +190,7 @@ def tile_picked_anc8_silu_po_kernel(
             z_codes = tile([P, PIECE], U32, "z_codes%d" % c)
             z_scales = tile([P, PIECE], U8, "z_scales%d" % c)
             nc.vector.quantize_mx(z_codes[:].bitcast(FP8X4), z_scales[:], z_bf[:].rearrange("p n t -> p (n t)"))
-            acc = ps.tile([P, PACK, PIECE], F32, name="acc%d" % c, tag="bank%d" % (PIECES + c))
+            acc = ps.tile([P, PACK, PIECE], F32, name="acc%d" % c, tag="bank%d" % (PACK + c))
             for t in range(PACK):
                 cols = slice(t * P, (t + 1) * P)
                 nc.tensor.matmul_mx(

@@ -72,27 +72,27 @@ def tile_picked_anc8_silu_po_kernel(
         nc.sync.dma_start(w1_raw[0][:], w1_rows[0])
         nc.sync.dma_start(table[2][:, :U], emb_rows[2])
         nc.sync.dma_start(table[3][:, :U], emb_rows[3])
+        for q in range(QUADS):
+            nc.sync.dma_start(
+                w2s_raw[32 * q : 32 * q + 4, :].bitcast(I32), w2_scales[0, 4 * q : 4 * q + 4, :].bitcast(I32)
+            )
+        nc.sync.dma_start(w1_raw[1][:], w1_rows[1])
         nc.sync.dma_start(picked[:], offs)
         for q in range(QUADS):
             nc.sync.dma_start(
                 xs_all[32 * q : 32 * q + 4 * PASSES, :].bitcast(I32), x_scales[:, 4 * q : 4 * q + 4, :].bitcast(I32)
             )
-        nc.sync.dma_start(w1_raw[1][:], w1_rows[1])
         load_x(0)
-        for q in range(QUADS):
-            nc.sync.dma_start(
-                w2s_raw[32 * q : 32 * q + 4, :].bitcast(I32), w2_scales[0, 4 * q : 4 * q + 4, :].bitcast(I32)
-            )
         load_x(1)
         nc.sync.dma_start(w2_raw[:], w2_words[0].rearrange("p n t -> p (n t)").bitcast(I32))
 
-        e_turned = tile([P, PACK, PIECES, P], F32, "e_turned")
+        e_sum = []
         for t in range(PACK):
             bank = ps.tile([P, PIECES, P], F32, name="e_sum%d" % t, tag="bank%d" % t)
             for n in range(LISTS):
                 got = tile([P, S], F32, "got%d_%d" % (t, n))
                 step = LISTS * t + n
-                if step % 2 and step < 8:
+                if step % 2 and step < 10:
                     nc.vector.tensor_copy(got[:], table[t][:].indirect(lists[n][:]))
                 else:
                     nc.scalar.activation(got[:], table[t][:].indirect(lists[n][:]), COPY)
@@ -105,10 +105,7 @@ def tile_picked_anc8_silu_po_kernel(
                         start=n == 0 and c == 0,
                         stop=n == LISTS - 1 and c == PIECES - 1,
                     )
-            if t < 2:
-                nc.vector.tensor_copy(e_turned[:, t, :, :], bank[:])
-            else:
-                nc.scalar.copy(e_turned[:, t, :, :], bank[:])
+            e_sum.append(bank)
 
         w1_codes = [tile([P, H], U32, "w1_codes0"), None]
         w1_scales = [tile([P, H], U8, "w1_scales%d" % g) for g in range(PASSES)]
@@ -122,20 +119,23 @@ def tile_picked_anc8_silu_po_kernel(
 
         xs = tile([P, S], U8, "xs")
         xg0 = tile([P, S], U32, "xg0")
-        xg1 = [tile([P, HALF], U32, "xg1_%d" % h) for h in range(2)]
+        cuts = (0, PIECE, HALF, S)
+        xg1 = [tile([P, b - a], U32, "xg1_%d" % a) for a, b in zip(cuts, cuts[1:])]
         nc.vector.tensor_copy(xs[:], xs_all[:].indirect(picked[:]))
         nc.vector.tensor_copy(xg0[:], x_all[0][:].bitcast(U32).indirect(picked[:]))
         w1_codes[1] = tile([P, H], U32, "w1_codes1", "x_all0")
         quantise_w1(1)
+        e_turned = tile([P, PACK, PIECES, P], F32, "e_turned", "w1_raw1")
+        for t in range(PACK):
+            nc.scalar.copy(e_turned[:, t, :, :], e_sum[t][:])
         w2_codes = tile([P, N], U32, "w2_codes")
         w2_sc = tile([P, N], U8, "w2_sc")
         nc.vector.tensor_copy(
             w2_sc[:].rearrange("p (t m) -> p m t", t=PACK), w2s_raw[:].rearrange("p (m t) -> p m t", t=PACK)
         )
-        for h in range(2):
-            nc.vector.tensor_copy(
-                xg1[h][:], x_all[1][:].bitcast(U32).indirect(picked[:, h * HALF // 16 : (h + 1) * HALF // 16])
-            )
+        for dst, a, b in zip(xg1, cuts, cuts[1:]):
+            nc.vector.tensor_copy(dst[:], x_all[1][:].bitcast(U32).indirect(picked[:, a // 16 : b // 16]))
+        late = [xg1[0][:], xg1[1][:], xg1[2][:, :PIECE], xg1[2][:, PIECE:]]
         nc.scalar.copy(
             w2_codes[:].rearrange("p (t m) -> p m t", t=PACK),
             w2_raw[:].bitcast(U32).rearrange("p (m t) -> p m t", t=PACK),
@@ -147,7 +147,7 @@ def tile_picked_anc8_silu_po_kernel(
                 cols = slice(c * PIECE, (c + 1) * PIECE)
                 nc.tensor.matmul_mx(
                     y[c][:],
-                    lhsT=(xg1[c // 2][:, c % 2 * PIECE : (c % 2 + 1) * PIECE] if g else xg0[:, cols]).bitcast(FP8X4),
+                    lhsT=(late[c] if g else xg0[:, cols]).bitcast(FP8X4),
                     lhsT_scale=xs[4 * g : P, cols],
                     rhs=w1_codes[g][:].bitcast(FP8X4),
                     rhs_scale=w1_scales[g][:],
@@ -206,9 +206,14 @@ def tile_picked_anc8_silu_po_kernel(
 
         def store(c, acc, o_bf):
             o_f32 = tile([P, PACK, PIECE], F32, "o_f32%d" % c)
-            nc.scalar.copy(o_f32[:], acc[:])
+            if c == 3:
+                nc.vector.tensor_copy(woven(o_bf), planar(acc[:]))
+            (nc.vector.tensor_copy if c == 0 else nc.scalar.copy)(o_f32[:], acc[:])
             nc.sync.dma_start(out_rows[:, :, c * PIECE : (c + 1) * PIECE], o_f32[:])
-            nc.vector.tensor_copy(woven(o_bf), planar(o_f32[:]))
+            if c == 0:
+                nc.gpsimd.tensor_scalar(o_bf, o_f32[:].rearrange("p t n -> p n t"), 1.0, -0.0, MULT, ADD)
+            elif c < 3:
+                nc.vector.tensor_copy(woven(o_bf), planar(o_f32[:]))
 
         def hand_on(half, o_bf):
             o_codes = tile([P, HALF], I32, "o_codes%d" % half)

@@ -86,26 +86,27 @@ def tile_picked_anc8_silu_po_kernel(
         load_x(1)
         nc.sync.dma_start(w2_raw[:], w2_words[0].rearrange("p n t -> p (n t)").bitcast(I32))
 
-        e_sum = []
+        e_sum = [ps.tile([P, PACK, P], F32, name="e_sum%d" % c, tag="bank%d" % c) for c in range(PIECES)]
         for t in range(PACK):
-            bank = ps.tile([P, PIECES, P], F32, name="e_sum%d" % t, tag="bank%d" % t)
             for n in range(LISTS):
                 got = tile([P, S], F32, "got%d_%d" % (t, n))
                 step = LISTS * t + n
-                if step % 2 and step < 10:
+                if step % 2 and step < 8:
                     nc.vector.tensor_copy(got[:], table[t][:].indirect(lists[n][:]))
                 else:
                     nc.scalar.activation(got[:], table[t][:].indirect(lists[n][:]), COPY)
                 for c in range(PIECES):
                     nc.tensor.matmul(
-                        bank[:, c, :],
+                        e_sum[c][:, t, :],
                         lhsT=got[:, c * PIECE : (c + 1) * PIECE],
                         rhs=ident[:],
                         is_transpose=True,
-                        start=n == 0 and c == 0,
-                        stop=n == LISTS - 1 and c == PIECES - 1,
+                        start=step == 0,
+                        stop=step == PACK * LISTS - 1,
                     )
-            e_sum.append(bank)
+        e_turned = [tile([P, PACK, P], F32, "e_turned%d" % c) for c in range(PIECES)]
+        for c in range(PIECES):
+            nc.scalar.copy(e_turned[c][:], e_sum[c][:])
 
         w1_codes = [tile([P, H], U32, "w1_codes0"), None]
         w1_scales = [tile([P, H], U8, "w1_scales%d" % g) for g in range(PASSES)]
@@ -125,9 +126,6 @@ def tile_picked_anc8_silu_po_kernel(
         nc.vector.tensor_copy(xg0[:], x_all[0][:].bitcast(U32).indirect(picked[:]))
         w1_codes[1] = tile([P, H], U32, "w1_codes1", "x_all0")
         quantise_w1(1)
-        e_turned = tile([P, PACK, PIECES, P], F32, "e_turned", "w1_raw1")
-        for t in range(PACK):
-            nc.scalar.copy(e_turned[:, t, :, :], e_sum[t][:])
         w2_codes = tile([P, N], U32, "w2_codes")
         w2_sc = tile([P, N], U8, "w2_sc")
         nc.vector.tensor_copy(
@@ -136,24 +134,30 @@ def tile_picked_anc8_silu_po_kernel(
         for dst, a, b in zip(xg1, cuts, cuts[1:]):
             nc.vector.tensor_copy(dst[:], x_all[1][:].bitcast(U32).indirect(picked[:, a // 16 : b // 16]))
         late = [xg1[0][:], xg1[1][:], xg1[2][:, :PIECE], xg1[2][:, PIECE:]]
-        nc.scalar.copy(
-            w2_codes[:].rearrange("p (t m) -> p m t", t=PACK),
-            w2_raw[:].bitcast(U32).rearrange("p (m t) -> p m t", t=PACK),
+        nc.gpsimd.tensor_copy(
+            w2_codes[:].rearrange("p (t m) -> p t m", t=PACK),
+            w2_raw[:].bitcast(U32).rearrange("p (m t) -> p t m", t=PACK),
         )
 
-        y = [ps.tile([P, H], F32, name="y%d" % c, tag="bank%d" % (PACK + c)) for c in range(PIECES)]
+        y = {}
+
+        def first_layer(c, g):
+            if g == 0:
+                y[c] = ps.tile([P, H], F32, name="y%d" % c, tag="bank%d" % (PACK + c % 3))
+            cols = slice(c * PIECE, (c + 1) * PIECE)
+            nc.tensor.matmul_mx(
+                y[c][:],
+                lhsT=(late[c] if g else xg0[:, cols]).bitcast(FP8X4),
+                lhsT_scale=xs[4 * g : P, cols],
+                rhs=w1_codes[g][:].bitcast(FP8X4),
+                rhs_scale=w1_scales[g][:],
+                start=g == 0,
+                stop=g == PASSES - 1,
+            )
+
         for g in range(PASSES):
-            for c in range(PIECES):
-                cols = slice(c * PIECE, (c + 1) * PIECE)
-                nc.tensor.matmul_mx(
-                    y[c][:],
-                    lhsT=(late[c] if g else xg0[:, cols]).bitcast(FP8X4),
-                    lhsT_scale=xs[4 * g : P, cols],
-                    rhs=w1_codes[g][:].bitcast(FP8X4),
-                    rhs_scale=w1_scales[g][:],
-                    start=g == 0,
-                    stop=g == PASSES - 1,
-                )
+            for c in range(PIECES - 1):
+                first_layer(c, g)
 
         out_rows = out_0.rearrange("(p t) j -> p t j", t=PACK)
         out_words = out_1[0].rearrange("p n t -> p (n t)").bitcast(I32)
@@ -180,17 +184,17 @@ def tile_picked_anc8_silu_po_kernel(
             u = ps.tile([P, PACK, PIECE], F32, name="u%d" % c, tag="bank%d" % c)
             y_dealt = y[c][:].rearrange("j (p t) -> j t p", t=PACK)
             turned = tile([P, PACK, P], F32, "turned%d" % c)
-            nc.vector.tensor_tensor(turned[:], y_dealt, e_turned[:, :, c, :], ADD)
+            nc.vector.tensor_tensor(turned[:], y_dealt, e_turned[c][:], ADD)
             turn(u, turned, True, True)
             z_bf = tile([P, PIECE, PACK], BF16, "z%d" % c)
-            nc.scalar.activation(woven(z_bf[:]), planar(u[:]), SILU)
+            nc.scalar.activation(z_bf[:], u[:].rearrange("p t n -> p n t"), SILU)
             return z_bf
 
         def second_layer(c, z_bf):
             z_codes = tile([P, PIECE], U32, "z_codes%d" % c)
             z_scales = tile([P, PIECE], U8, "z_scales%d" % c)
             nc.vector.quantize_mx(z_codes[:].bitcast(FP8X4), z_scales[:], z_bf[:].rearrange("p n t -> p (n t)"))
-            acc = ps.tile([P, PACK, PIECE], F32, name="acc%d" % c, tag="bank%d" % (PACK + c))
+            acc = ps.tile([P, PACK, PIECE], F32, name="acc%d" % c, tag="bank%d" % (PACK + (c + 3) % 4))
             for t in range(PACK):
                 cols = slice(t * P, (t + 1) * P)
                 nc.tensor.matmul_mx(
@@ -207,7 +211,7 @@ def tile_picked_anc8_silu_po_kernel(
         def store(c, acc, o_bf):
             o_f32 = tile([P, PACK, PIECE], F32, "o_f32%d" % c)
             if c == 3:
-                nc.vector.tensor_copy(woven(o_bf), planar(acc[:]))
+                nc.vector.tensor_copy(o_bf, acc[:].rearrange("p t n -> p n t"))
             (nc.vector.tensor_copy if c == 0 else nc.scalar.copy)(o_f32[:], acc[:])
             nc.sync.dma_start(out_rows[:, :, c * PIECE : (c + 1) * PIECE], o_f32[:])
             if c == 0:
@@ -221,7 +225,10 @@ def tile_picked_anc8_silu_po_kernel(
             nc.vector.quantize_mx(o_codes[:].bitcast(FP8X4), o_scales[:, cols], o_bf[:].rearrange("p n t -> p (n t)"))
             nc.sync.dma_start(out_words[:, cols], o_codes[:])
 
-        z = [hidden(c) for c in range(PIECES)]
+        z = [hidden(0)]
+        for g in range(PASSES):
+            first_layer(PIECES - 1, g)
+        z.extend(hidden(c) for c in range(1, PIECES))
         accs = [second_layer(c, z[c]) for c in range(PIECES)]
         for half in range(2):
             o_bf = tile([P, HALF, PACK], BF16, "o_bf%d" % half)

@@ -134,16 +134,16 @@ def tile_picked_anc8_silu_po_kernel(
         for dst, a, b in zip(xg1, cuts, cuts[1:]):
             nc.vector.tensor_copy(dst[:], x_all[1][:].bitcast(U32).indirect(picked[:, a // 16 : b // 16]))
         late = [xg1[0][:], xg1[1][:], xg1[2][:, :PIECE], xg1[2][:, PIECE:]]
-        nc.gpsimd.tensor_copy(
-            w2_codes[:].rearrange("p (t m) -> p t m", t=PACK),
-            w2_raw[:].bitcast(U32).rearrange("p (m t) -> p t m", t=PACK),
+        nc.scalar.copy(
+            w2_codes[:].rearrange("p (t m) -> p m t", t=PACK),
+            w2_raw[:].bitcast(U32).rearrange("p (m t) -> p m t", t=PACK),
         )
 
         y = {}
 
         def first_layer(c, g):
             if g == 0:
-                y[c] = ps.tile([P, H], F32, name="y%d" % c, tag="bank%d" % (PACK + c % 3))
+                y[c] = ps.tile([P, H], F32, name="y%d" % c, tag="bank%d" % (PACK + c))
             cols = slice(c * PIECE, (c + 1) * PIECE)
             nc.tensor.matmul_mx(
                 y[c][:],
@@ -156,7 +156,7 @@ def tile_picked_anc8_silu_po_kernel(
             )
 
         for g in range(PASSES):
-            for c in range(PIECES - 1):
+            for c in range(PIECES):
                 first_layer(c, g)
 
         out_rows = out_0.rearrange("(p t) j -> p t j", t=PACK)
@@ -194,7 +194,7 @@ def tile_picked_anc8_silu_po_kernel(
             z_codes = tile([P, PIECE], U32, "z_codes%d" % c)
             z_scales = tile([P, PIECE], U8, "z_scales%d" % c)
             nc.vector.quantize_mx(z_codes[:].bitcast(FP8X4), z_scales[:], z_bf[:].rearrange("p n t -> p (n t)"))
-            acc = ps.tile([P, PACK, PIECE], F32, name="acc%d" % c, tag="bank%d" % (PACK + (c + 3) % 4))
+            acc = ps.tile([P, PACK, PIECE], F32, name="acc%d" % c, tag="bank%d" % (PACK + c))
             for t in range(PACK):
                 cols = slice(t * P, (t + 1) * P)
                 nc.tensor.matmul_mx(
@@ -214,9 +214,7 @@ def tile_picked_anc8_silu_po_kernel(
                 nc.vector.tensor_copy(o_bf, acc[:].rearrange("p t n -> p n t"))
             (nc.vector.tensor_copy if c == 0 else nc.scalar.copy)(o_f32[:], acc[:])
             nc.sync.dma_start(out_rows[:, :, c * PIECE : (c + 1) * PIECE], o_f32[:])
-            if c == 0:
-                nc.gpsimd.tensor_scalar(o_bf, o_f32[:].rearrange("p t n -> p n t"), 1.0, -0.0, MULT, ADD)
-            elif c < 3:
+            if c < 3:
                 nc.vector.tensor_copy(woven(o_bf), planar(o_f32[:]))
 
         def hand_on(half, o_bf):
@@ -225,10 +223,7 @@ def tile_picked_anc8_silu_po_kernel(
             nc.vector.quantize_mx(o_codes[:].bitcast(FP8X4), o_scales[:, cols], o_bf[:].rearrange("p n t -> p (n t)"))
             nc.sync.dma_start(out_words[:, cols], o_codes[:])
 
-        z = [hidden(0)]
-        for g in range(PASSES):
-            first_layer(PIECES - 1, g)
-        z.extend(hidden(c) for c in range(1, PIECES))
+        z = [hidden(c) for c in range(PIECES)]
         accs = [second_layer(c, z[c]) for c in range(PIECES)]
         for half in range(2):
             o_bf = tile([P, HALF, PACK], BF16, "o_bf%d" % half)

@@ -34,18 +34,20 @@ def tile_picked_anc8_silu_po_kernel(
     nc = tc.nc
     with ExitStack() as ctx:
         sb = ctx.enter_context(tc.tile_pool(name="sb", bufs=1))
+        relay = ctx.enter_context(tc.tile_pool(name="relay", bufs=1))
         ps = ctx.enter_context(tc.psum_pool(name="ps", bufs=1))
 
         def tile(shape, dtype, name, tag=None):
             return sb.tile(shape, dtype, name=name, tag=tag or name, align_bytes=64)
 
+        def placed(shape, dtype, name, offset):
+            return relay.tile(shape, dtype, name=name, offset=offset, align_bytes=64)
+
         lists = [tile([P, S // 16], U16, "up%d" % n) for n in range(LISTS)]
         picked = tile([P, S // 16], U16, "picked")
         table = [tile([P, 2 * U], F32, "table%d" % t) for t in range(PACK)]
         w1_raw = [tile([P, PACK, H], F32, "w1_raw%d" % g) for g in range(PASSES)]
-        x_all = [tile([P, T], I32, "x_all%d" % g) for g in range(PASSES)]
         xs_all = tile([P, T], U8, "xs_all")
-        w2_raw = tile([P, N], I32, "w2_raw")
         w2s_raw = tile([P, N], U8, "w2s_raw")
         ident = tile([P, P], F32, "ident")
 
@@ -61,30 +63,33 @@ def tile_picked_anc8_silu_po_kernel(
         emb_rows = emb.rearrange("(p t) u -> t p u", t=PACK)
         w1_rows = w1.rearrange("(g p j) c -> g p j c", p=P, j=PACK)
 
-        def load_x(g):
-            nc.sync.dma_start(x_all[g][:], x_words[g].rearrange("p n t -> p (n t)").bitcast(I32))
-
         nc.sync.dma_start(table[0][:, :U], emb_rows[0])
         nc.sync.dma_start(lists[0][:], up1)
         nc.sync.dma_start(lists[1][:], up2)
+        nc.sync.dma_start(picked[:], offs)
         nc.sync.dma_start(lists[2][:], up3)
+        nc.sync.dma_start(xs_all[0:P:4, :].bitcast(I32), x_scales.rearrange("g a n -> a g n").bitcast(I32))
         nc.sync.dma_start(table[1][:, :U], emb_rows[1])
         nc.sync.dma_start(w1_raw[0][:], w1_rows[0])
         nc.sync.dma_start(table[2][:, :U], emb_rows[2])
         nc.sync.dma_start(table[3][:, :U], emb_rows[3])
+        nc.sync.dma_start(w1_raw[1][:], w1_rows[1])
         for q in range(QUADS):
-            nc.sync.dma_start(
+            nc.gpsimd.dma_start(
                 w2s_raw[32 * q : 32 * q + 4, :].bitcast(I32), w2_scales[0, 4 * q : 4 * q + 4, :].bitcast(I32)
             )
-        nc.sync.dma_start(w1_raw[1][:], w1_rows[1])
-        nc.sync.dma_start(picked[:], offs)
-        for q in range(QUADS):
-            nc.sync.dma_start(
-                xs_all[32 * q : 32 * q + 4 * PASSES, :].bitcast(I32), x_scales[:, 4 * q : 4 * q + 4, :].bitcast(I32)
-            )
-        load_x(0)
-        load_x(1)
-        nc.sync.dma_start(w2_raw[:], w2_words[0].rearrange("p n t -> p (n t)").bitcast(I32))
+
+        xs_spread = placed([P, S], U8, "xs_spread", 4 * T - S // 2)
+        xs = tile([P, S], U8, "xs")
+        nc.vector.tensor_copy(xs_spread[:], xs_all[:].indirect(picked[:]))
+        nc.vector.tensor_copy(xs[:].bitcast(I32), xs_spread[:].bitcast(I32))
+        x_all = [placed([P, T], I32, "x_all%d" % g, 4 * T * g) for g in range(PASSES)]
+        for g in range(PASSES):
+            for r in range(1, 4):
+                nc.sync.dma_start(
+                    xs[4 * g + r : P : 32, :].bitcast(I32), xs[4 * g + 8 * r : P : 32, :].bitcast(I32)
+                )
+            nc.sync.dma_start(x_all[g][:], x_words[g].rearrange("p n t -> p (n t)").bitcast(I32))
 
         e_sum = [ps.tile([P, PACK, P], F32, name="e_sum%d" % c, tag="bank%d" % c) for c in range(PIECES)]
         for t in range(PACK):
@@ -117,14 +122,14 @@ def tile_picked_anc8_silu_po_kernel(
             nc.vector.quantize_mx(w1_codes[g][:].bitcast(FP8X4), w1_scales[g][:], w1_bf[:].rearrange("p c j -> p (c j)"))
 
         quantise_w1(0)
+        w2_raw = tile([P, N], I32, "w2_raw", "w1_raw0")
+        nc.sync.dma_start(w2_raw[:], w2_words[0].rearrange("p n t -> p (n t)").bitcast(I32))
 
-        xs = tile([P, S], U8, "xs")
         xg0 = tile([P, S], U32, "xg0")
         cuts = (0, PIECE, HALF, S)
         xg1 = [tile([P, b - a], U32, "xg1_%d" % a) for a, b in zip(cuts, cuts[1:])]
-        nc.vector.tensor_copy(xs[:], xs_all[:].indirect(picked[:]))
         nc.vector.tensor_copy(xg0[:], x_all[0][:].bitcast(U32).indirect(picked[:]))
-        w1_codes[1] = tile([P, H], U32, "w1_codes1", "x_all0")
+        w1_codes[1] = placed([P, H], U32, "w1_codes1", 0)
         quantise_w1(1)
         w2_codes = tile([P, N], U32, "w2_codes")
         w2_sc = tile([P, N], U8, "w2_sc")

@@ -96,7 +96,7 @@ def tile_picked_anc8_silu_po_kernel(
             for n in range(LISTS):
                 got = tile([P, S], F32, "got%d_%d" % (t, n))
                 step = LISTS * t + n
-                if step % 2 and step < 8:
+                if step % 2 and step < 10:
                     nc.vector.tensor_copy(got[:], table[t][:].indirect(lists[n][:]))
                 else:
                     nc.scalar.activation(got[:], table[t][:].indirect(lists[n][:]), COPY)
@@ -117,24 +117,37 @@ def tile_picked_anc8_silu_po_kernel(
         w1_scales = [tile([P, H], U8, "w1_scales%d" % g) for g in range(PASSES)]
 
         def quantise_w1(g):
-            w1_bf = tile([P, H, PACK], BF16, "w1_bf%d" % g, "w1_bf")
-            nc.gpsimd.tensor_scalar(w1_bf[:], w1_raw[g][:].rearrange("p j c -> p c j"), 1.0, 0.0, MULT, ADD)
+            w1_bf = tile([P, H, PACK], BF16, "w1_bf%d" % g)
+            width = H // (g + 1)
+            for a in range(0, H, width):
+                nc.gpsimd.tensor_scalar(
+                    w1_bf[:, a : a + width, :],
+                    w1_raw[g][:, :, a : a + width].rearrange("p j c -> p c j"),
+                    1.0,
+                    0.0,
+                    MULT,
+                    ADD,
+                )
             nc.vector.quantize_mx(w1_codes[g][:].bitcast(FP8X4), w1_scales[g][:], w1_bf[:].rearrange("p c j -> p (c j)"))
 
         quantise_w1(0)
         w2_raw = tile([P, N], I32, "w2_raw", "w1_raw0")
         nc.sync.dma_start(w2_raw[:], w2_words[0].rearrange("p n t -> p (n t)").bitcast(I32))
 
-        xg0 = tile([P, S], U32, "xg0")
+        xg0 = [tile([P, HALF], U32, "xg0_%d" % h) for h in range(2)]
         cuts = (0, PIECE, HALF, S)
         xg1 = [tile([P, b - a], U32, "xg1_%d" % a) for a, b in zip(cuts, cuts[1:])]
-        nc.vector.tensor_copy(xg0[:], x_all[0][:].bitcast(U32).indirect(picked[:]))
+        for h in range(2):
+            nc.vector.tensor_copy(
+                xg0[h][:], x_all[0][:].bitcast(U32).indirect(picked[:, h * HALF // 16 : (h + 1) * HALF // 16])
+            )
+        early = [xg0[c // 2][:, c % 2 * PIECE : (c % 2 + 1) * PIECE] for c in range(PIECES)]
         w1_codes[1] = placed([P, H], U32, "w1_codes1", 0)
         quantise_w1(1)
         w2_codes = tile([P, N], U32, "w2_codes")
-        w2_sc = tile([P, N], U8, "w2_sc")
-        nc.vector.tensor_copy(
-            w2_sc[:].rearrange("p (t m) -> p m t", t=PACK), w2s_raw[:].rearrange("p (m t) -> p m t", t=PACK)
+        w2_sc = tile([P, N], U8, "w2_sc", "w1_bf1")
+        nc.gpsimd.tensor_copy(
+            w2_sc[:].rearrange("p (t m) -> p t m", t=PACK), w2s_raw[:].rearrange("p (m t) -> p t m", t=PACK)
         )
         for dst, a, b in zip(xg1, cuts, cuts[1:]):
             nc.vector.tensor_copy(dst[:], x_all[1][:].bitcast(U32).indirect(picked[:, a // 16 : b // 16]))
@@ -152,7 +165,7 @@ def tile_picked_anc8_silu_po_kernel(
             cols = slice(c * PIECE, (c + 1) * PIECE)
             nc.tensor.matmul_mx(
                 y[c][:],
-                lhsT=(late[c] if g else xg0[:, cols]).bitcast(FP8X4),
+                lhsT=(late if g else early)[c].bitcast(FP8X4),
                 lhsT_scale=xs[4 * g : P, cols],
                 rhs=w1_codes[g][:].bitcast(FP8X4),
                 rhs_scale=w1_scales[g][:],

@@ -80,16 +80,22 @@ def tile_picked_anc8_silu_po_kernel(
             )
 
         xs_spread = placed([P, S], U8, "xs_spread", 4 * T - S // 2)
-        xs = tile([P, S], U8, "xs")
         nc.vector.tensor_copy(xs_spread[:], xs_all[:].indirect(picked[:]))
-        nc.vector.tensor_copy(xs[:].bitcast(I32), xs_spread[:].bitcast(I32))
-        x_all = [placed([P, T], I32, "x_all%d" % g, 4 * T * g) for g in range(PASSES)]
+        xs = [tile([P, S], U8, "xs%d" % g) for g in range(PASSES)]
         for g in range(PASSES):
+            nc.vector.tensor_copy(xs[g][:].bitcast(I32), xs_spread[:].bitcast(I32))
+        x_all = [placed([P, T], I32, "x_all%d" % g, 4 * T * g) for g in range(PASSES)]
+
+        def place_rows(g):
             for r in range(1, 4):
                 nc.sync.dma_start(
-                    xs[4 * g + r : P : 32, :].bitcast(I32), xs[4 * g + 8 * r : P : 32, :].bitcast(I32)
+                    xs[g][4 * g + r : P : 32, :].bitcast(I32), xs[g][4 * g + 8 * r : P : 32, :].bitcast(I32)
                 )
+
+        place_rows(0)
+        for g in range(PASSES):
             nc.sync.dma_start(x_all[g][:], x_words[g].rearrange("p n t -> p (n t)").bitcast(I32))
+        place_rows(1)
 
         e_sum = [ps.tile([P, PACK, P], F32, name="e_sum%d" % c, tag="bank%d" % c) for c in range(PIECES)]
         for t in range(PACK):
@@ -166,7 +172,7 @@ def tile_picked_anc8_silu_po_kernel(
             nc.tensor.matmul_mx(
                 y[c][:],
                 lhsT=(late if g else early)[c].bitcast(FP8X4),
-                lhsT_scale=xs[4 * g : P, cols],
+                lhsT_scale=xs[g][4 * g : P, cols],
                 rhs=w1_codes[g][:].bitcast(FP8X4),
                 rhs_scale=w1_scales[g][:],
                 start=g == 0,

@@ -206,9 +206,13 @@ def tile_picked_anc8_silu_po_kernel(
 
         def hidden(c):
             u = ps.tile([P, PACK, PIECE], F32, name="u%d" % c, tag="bank%d" % c)
-            y_dealt = y[c][:].rearrange("j (p t) -> j t p", t=PACK)
             turned = tile([P, PACK, P], F32, "turned%d" % c)
-            nc.vector.tensor_tensor(turned[:], y_dealt, e_turned[c][:], ADD)
+            nc.vector.tensor_tensor(
+                turned[:].rearrange("j t (b q) -> j b t q", q=4),
+                y[c][:].rearrange("j (b q t) -> j b t q", q=4, t=PACK),
+                e_turned[c][:].rearrange("j t (b q) -> j b t q", q=4),
+                ADD,
+            )
             turn(u, turned, True, True)
             z_bf = tile([P, PIECE, PACK], BF16, "z%d" % c)
             nc.scalar.activation(z_bf[:], u[:].rearrange("p t n -> p n t"), SILU)

@@ -47,13 +47,16 @@ def tile_picked_anc8_silu_po_kernel(
         picked = tile([P, S // 16], U16, "picked")
         table = [tile([P, 2 * U], F32, "table%d" % t) for t in range(PACK)]
         w1_raw = [tile([P, PACK, H], F32, "w1_raw%d" % g) for g in range(PASSES)]
-        xs_all = tile([P, T], U8, "xs_all")
+        xs_all = placed([P, T], U8, "xs_all", 4 * T - T // 2)
+        xs = [tile([P, S], U8, "xs%d" % g) for g in range(PASSES)]
         w2s_raw = tile([P, N], U8, "w2s_raw")
         ident = tile([P, P], F32, "ident")
 
         nc.gpsimd.memset(xs_all[:].bitcast(I32), 0)
         nc.gpsimd.memset(w2s_raw[:].bitcast(I32), 0)
         make_identity(nc, ident[:])
+        for g in range(PASSES):
+            nc.vector.memset(xs[g][:].bitcast(I32), 0)
 
         idle_in = tile([P, 1], F32, "idle_in")
         idle_out = tile([P, 1], F32, "idle_out")
@@ -79,18 +82,13 @@ def tile_picked_anc8_silu_po_kernel(
                 w2s_raw[32 * q : 32 * q + 4, :].bitcast(I32), w2_scales[0, 4 * q : 4 * q + 4, :].bitcast(I32)
             )
 
-        xs_spread = placed([P, S], U8, "xs_spread", 4 * T - S // 2)
+        xs_spread = tile([P, S], U8, "xs_spread")
         nc.vector.tensor_copy(xs_spread[:], xs_all[:].indirect(picked[:]))
-        xs = [tile([P, S], U8, "xs%d" % g) for g in range(PASSES)]
-        for g in range(PASSES):
-            nc.vector.tensor_copy(xs[g][:].bitcast(I32), xs_spread[:].bitcast(I32))
         x_all = [placed([P, T], I32, "x_all%d" % g, 4 * T * g) for g in range(PASSES)]
 
         def place_rows(g):
-            for r in range(1, 4):
-                nc.sync.dma_start(
-                    xs[g][4 * g + r : P : 32, :].bitcast(I32), xs[g][4 * g + 8 * r : P : 32, :].bitcast(I32)
-                )
+            for r in range(4):
+                nc.sync.dma_start(xs[g][r:P:32, :].bitcast(I32), xs_spread[4 * g + 8 * r : P : 32, :].bitcast(I32))
 
         place_rows(0)
         for g in range(PASSES):
@@ -98,26 +96,31 @@ def tile_picked_anc8_silu_po_kernel(
         place_rows(1)
 
         e_sum = [ps.tile([P, PACK, P], F32, name="e_sum%d" % c, tag="bank%d" % c) for c in range(PIECES)]
-        for t in range(PACK):
-            for n in range(LISTS):
-                got = tile([P, S], F32, "got%d_%d" % (t, n))
-                step = LISTS * t + n
-                if step % 2 and step < 10:
-                    nc.vector.tensor_copy(got[:], table[t][:].indirect(lists[n][:]))
-                else:
-                    nc.scalar.activation(got[:], table[t][:].indirect(lists[n][:]), COPY)
-                for c in range(PIECES):
-                    nc.tensor.matmul(
-                        e_sum[c][:, t, :],
-                        lhsT=got[:, c * PIECE : (c + 1) * PIECE],
-                        rhs=ident[:],
-                        is_transpose=True,
-                        start=step == 0,
-                        stop=step == PACK * LISTS - 1,
-                    )
-        e_turned = [tile([P, PACK, P], F32, "e_turned%d" % c) for c in range(PIECES)]
-        for c in range(PIECES):
-            nc.scalar.copy(e_turned[c][:], e_sum[c][:])
+
+        def look_up(step, on_vector, first, last, closes, tag=None):
+            t, n = divmod(step, LISTS)
+            got = tile([P, (last - first) * PIECE], F32, "got%d_%d" % (step, first), tag)
+            window = table[t][:].indirect(lists[n][:, first * PIECE // 16 : last * PIECE // 16])
+            if on_vector:
+                nc.vector.tensor_copy(got[:], window)
+            else:
+                nc.scalar.activation(got[:], window, COPY)
+            for c in range(first, last):
+                nc.tensor.matmul(
+                    e_sum[c][:, t, :],
+                    lhsT=got[:, (c - first) * PIECE : (c - first + 1) * PIECE],
+                    rhs=ident[:],
+                    is_transpose=True,
+                    start=step == 0,
+                    stop=c in closes,
+                )
+
+        for step in range(PACK * LISTS):
+            if step == 5:
+                look_up(step, False, 0, 2, ())
+                look_up(step, True, 2, PIECES, ())
+            else:
+                look_up(step, step % 2 and step < 10, 0, PIECES, range(PIECES) if step == PACK * LISTS - 1 else ())
 
         w1_codes = [tile([P, H], U32, "w1_codes0"), None]
         w1_scales = [tile([P, H], U8, "w1_scales%d" % g) for g in range(PASSES)]
@@ -137,6 +140,9 @@ def tile_picked_anc8_silu_po_kernel(
             nc.vector.quantize_mx(w1_codes[g][:].bitcast(FP8X4), w1_scales[g][:], w1_bf[:].rearrange("p c j -> p (c j)"))
 
         quantise_w1(0)
+        e_turned = [tile([P, PACK, P], F32, "e_turned%d" % c) for c in range(PIECES)]
+        for c in range(PIECES):
+            nc.scalar.copy(e_turned[c][:], e_sum[c][:])
         w2_raw = tile([P, N], I32, "w2_raw", "w1_raw0")
         nc.sync.dma_start(w2_raw[:], w2_words[0].rearrange("p n t -> p (n t)").bitcast(I32))
 
@@ -172,7 +178,7 @@ def tile_picked_anc8_silu_po_kernel(
             nc.tensor.matmul_mx(
                 y[c][:],
                 lhsT=(late if g else early)[c].bitcast(FP8X4),
-                lhsT_scale=xs[g][4 * g : P, cols],
+                lhsT_scale=xs[g][:, cols],
                 rhs=w1_codes[g][:].bitcast(FP8X4),
                 rhs_scale=w1_scales[g][:],
                 start=g == 0,

@@ -119,8 +119,11 @@ def tile_picked_anc8_silu_po_kernel(
             if step == 5:
                 look_up(step, False, 0, 2, ())
                 look_up(step, True, 2, PIECES, ())
+            elif step == PACK * LISTS - 1:
+                look_up(step, False, 0, 2, range(PIECES))
+                look_up(step, False, 2, PIECES, range(PIECES))
             else:
-                look_up(step, step % 2 and step < 10, 0, PIECES, range(PIECES) if step == PACK * LISTS - 1 else ())
+                look_up(step, step % 2, 0, PIECES, ())
 
         w1_codes = [tile([P, H], U32, "w1_codes0"), None]
         w1_scales = [tile([P, H], U8, "w1_scales%d" % g) for g in range(PASSES)]

from contextlib import ExitStack

import concourse.mybir as mybir
from concourse.masks import make_identity

K, T, S, N, H, U = 1024, 2048, 512, 512, 512, 512
FLOPS = 2 * K * H * S + 2 * H * N * S

F32 = mybir.dt.float32
BF16 = mybir.dt.bfloat16
I32 = mybir.dt.int32
U32 = mybir.dt.uint32
U16 = mybir.dt.uint16
U8 = mybir.dt.uint8
FP8X4 = mybir.dt.float8_e4m3fn_x4
ADD = mybir.AluOpType.add
MULT = mybir.AluOpType.mult
SILU = mybir.ActivationFunctionType.Silu
COPY = mybir.ActivationFunctionType.Copy

P = 128
PACK = 4
PASSES = K // (P * PACK)
PIECE = 128
PIECES = S // PIECE
HALF = 256
QUADS = 4
LISTS = 3


def tile_picked_anc8_silu_po_kernel(
    tc, x_words, x_scales, w1, emb, w2_words, w2_scales, offs, up1, up2, up3, out_0, out_1, out_2
):
    nc = tc.nc
    with ExitStack() as ctx:
        sb = ctx.enter_context(tc.tile_pool(name="sb", bufs=1))
        relay = ctx.enter_context(tc.tile_pool(name="relay", bufs=1))
        ps = ctx.enter_context(tc.psum_pool(name="ps", bufs=1))

        def tile(shape, dtype, name, tag=None):
            return sb.tile(shape, dtype, name=name, tag=tag or name, align_bytes=64)

        def placed(shape, dtype, name, offset):
            return relay.tile(shape, dtype, name=name, offset=offset, align_bytes=64)

        lists = [tile([P, S // 16], U16, "up%d" % n) for n in range(LISTS)]
        picked = tile([P, S // 16], U16, "picked")
        table = [tile([P, 2 * U], F32, "table%d" % t) for t in range(PACK)]
        w1_raw = [tile([P, PACK, H], F32, "w1_raw%d" % g) for g in range(PASSES)]
        xs_all = placed([P, T], U8, "xs_all", 4 * T - T // 2)
        xs = [tile([P, S], U8, "xs%d" % g) for g in range(PASSES)]
        w2s_raw = tile([P, N], U8, "w2s_raw")
        ident = tile([P, P], F32, "ident")

        nc.gpsimd.memset(xs_all[:].bitcast(I32), 0)
        nc.gpsimd.memset(w2s_raw[:].bitcast(I32), 0)
        make_identity(nc, ident[:])
        for g in range(PASSES):
            nc.vector.memset(xs[g][:].bitcast(I32), 0)

        idle_in = tile([P, 1], F32, "idle_in")
        idle_out = tile([P, 1], F32, "idle_out")
        nc.vector.memset(idle_in[:], 0.0)
        nc.scalar.activation(idle_out[:], idle_in[:], SILU)

        emb_rows = emb.rearrange("(p t) u -> t p u", t=PACK)
        w1_rows = w1.rearrange("(g p j) c -> g p j c", p=P, j=PACK)

        nc.sync.dma_start(table[0][:, :U], emb_rows[0])
        nc.sync.dma_start(lists[0][:], up1)
        nc.sync.dma_start(lists[1][:], up2)
        nc.sync.dma_start(picked[:], offs)
        nc.sync.dma_start(lists[2][:], up3)
        nc.sync.dma_start(xs_all[0:P:4, :].bitcast(I32), x_scales.rearrange("g a n -> a g n").bitcast(I32))
        nc.sync.dma_start(table[1][:, :U], emb_rows[1])
        nc.sync.dma_start(w1_raw[0][:], w1_rows[0])
        nc.sync.dma_start(table[2][:, :U], emb_rows[2])
        nc.sync.dma_start(table[3][:, :U], emb_rows[3])
        nc.sync.dma_start(w1_raw[1][:], w1_rows[1])
        for q in range(QUADS):
            nc.gpsimd.dma_start(
                w2s_raw[32 * q : 32 * q + 4, :].bitcast(I32), w2_scales[0, 4 * q : 4 * q + 4, :].bitcast(I32)
            )

        xs_spread = tile([P, S], U8, "xs_spread")
        nc.vector.tensor_copy(xs_spread[:], xs_all[:].indirect(picked[:]))
        x_all = [placed([P, T], I32, "x_all%d" % g, 4 * T * g) for g in range(PASSES)]

        def place_rows(g):
            for r in range(4):
                nc.sync.dma_start(xs[g][r:P:32, :].bitcast(I32), xs_spread[4 * g + 8 * r : P : 32, :].bitcast(I32))

        place_rows(0)
        for g in range(PASSES):
            nc.sync.dma_start(x_all[g][:], x_words[g].rearrange("p n t -> p (n t)").bitcast(I32))
        place_rows(1)

        e_sum = [ps.tile([P, PACK, P], F32, name="e_sum%d" % c, tag="bank%d" % c) for c in range(PIECES)]

        def look_up(step, on_vector, first, last, closes, tag=None):
            t, n = divmod(step, LISTS)
            got = tile([P, (last - first) * PIECE], F32, "got%d_%d" % (step, first), tag)
            window = table[t][:].indirect(lists[n][:, first * PIECE // 16 : last * PIECE // 16])
            if on_vector:
                nc.vector.tensor_copy(got[:], window)
            else:
                nc.scalar.activation(got[:], window, COPY)
            for c in range(first, last):
                nc.tensor.matmul(
                    e_sum[c][:, t, :],
                    lhsT=got[:, (c - first) * PIECE : (c - first + 1) * PIECE],
                    rhs=ident[:],
                    is_transpose=True,
                    start=step == 0,
                    stop=c in closes,
                )

        for step in range(PACK * LISTS):
            if step == 5:
                look_up(step, False, 0, 2, ())
                look_up(step, True, 2, PIECES, ())
            elif step == PACK * LISTS - 1:
                look_up(step, False, 0, 2, range(PIECES))
                look_up(step, False, 2, PIECES, range(PIECES))
            else:
                look_up(step, step % 2, 0, PIECES, ())

        w1_codes = [tile([P, H], U32, "w1_codes0"), None]
        w1_scales = [tile([P, H], U8, "w1_scales%d" % g) for g in range(PASSES)]

        def quantise_w1(g):
            w1_bf = tile([P, H, PACK], BF16, "w1_bf%d" % g)
            width = H // (g + 1)
            for a in range(0, H, width):
                nc.gpsimd.tensor_scalar(
                    w1_bf[:, a : a + width, :],
                    w1_raw[g][:, :, a : a + width].rearrange("p j c -> p c j"),
                    1.0,
                    0.0,
                    MULT,
                    ADD,
                )
            nc.vector.quantize_mx(w1_codes[g][:].bitcast(FP8X4), w1_scales[g][:], w1_bf[:].rearrange("p c j -> p (c j)"))

        quantise_w1(0)
        e_turned = [tile([P, PACK, P], F32, "e_turned%d" % c) for c in range(PIECES)]
        for c in range(PIECES):
            nc.scalar.copy(e_turned[c][:], e_sum[c][:])
        w2_raw = tile([P, N], I32, "w2_raw", "w1_raw0")
        nc.sync.dma_start(w2_raw[:], w2_words[0].rearrange("p n t -> p (n t)").bitcast(I32))

        xg0 = [tile([P, HALF], U32, "xg0_%d" % h) for h in range(2)]
        cuts = (0, PIECE, HALF, S)
        xg1 = [tile([P, b - a], U32, "xg1_%d" % a) for a, b in zip(cuts, cuts[1:])]
        for h in range(2):
            nc.vector.tensor_copy(
                xg0[h][:], x_all[0][:].bitcast(U32).indirect(picked[:, h * HALF // 16 : (h + 1) * HALF // 16])
            )
        early = [xg0[c // 2][:, c % 2 * PIECE : (c % 2 + 1) * PIECE] for c in range(PIECES)]
        w1_codes[1] = placed([P, H], U32, "w1_codes1", 0)
        quantise_w1(1)
        w2_codes = tile([P, N], U32, "w2_codes")
        w2_sc = tile([P, N], U8, "w2_sc", "w1_bf1")
        nc.gpsimd.tensor_copy(
            w2_sc[:].rearrange("p (t m) -> p t m", t=PACK), w2s_raw[:].rearrange("p (m t) -> p t m", t=PACK)
        )
        for dst, a, b in zip(xg1, cuts, cuts[1:]):
            nc.vector.tensor_copy(dst[:], x_all[1][:].bitcast(U32).indirect(picked[:, a // 16 : b // 16]))
        late = [xg1[0][:], xg1[1][:], xg1[2][:, :PIECE], xg1[2][:, PIECE:]]
        nc.scalar.copy(
            w2_codes[:].rearrange("p (t m) -> p m t", t=PACK),
            w2_raw[:].bitcast(U32).rearrange("p (m t) -> p m t", t=PACK),
        )

        y = {}

        def first_layer(c, g):
            if g == 0:
                y[c] = ps.tile([P, H], F32, name="y%d" % c, tag="bank%d" % (PACK + c))
            cols = slice(c * PIECE, (c + 1) * PIECE)
            nc.tensor.matmul_mx(
                y[c][:],
                lhsT=(late if g else early)[c].bitcast(FP8X4),
                lhsT_scale=xs[g][:, cols],
                rhs=w1_codes[g][:].bitcast(FP8X4),
                rhs_scale=w1_scales[g][:],
                start=g == 0,
                stop=g == PASSES - 1,
            )

        for g in range(PASSES):
            for c in range(PIECES):
                first_layer(c, g)

        out_rows = out_0.rearrange("(p t) j -> p t j", t=PACK)
        out_words = out_1[0].rearrange("p n t -> p (n t)").bitcast(I32)
        o_scales = tile([P, S], U8, "o_scales")

        def woven(dst):
            return dst.rearrange("p (c i) t -> p c t i", i=4)

        def planar(src):
            return src.rearrange("p t (c i) -> p c t i", i=4)

        def turn(dst, src, first, last):
            for t in range(PACK):
                nc.tensor.matmul(
                    dst[:, t, :],
                    lhsT=src[:, t, :],
                    rhs=ident[:],
                    is_transpose=True,
                    start=first and t == 0,
                    stop=last and t == PACK - 1,
                )

        def hidden(c):
            u = ps.tile([P, PACK, PIECE], F32, name="u%d" % c, tag="bank%d" % c)
            turned = tile([P, PACK, P], F32, "turned%d" % c)
            nc.vector.tensor_tensor(
                turned[:].rearrange("j t (b q) -> j b t q", q=4),
                y[c][:].rearrange("j (b q t) -> j b t q", q=4, t=PACK),
                e_turned[c][:].rearrange("j t (b q) -> j b t q", q=4),
                ADD,
            )
            turn(u, turned, True, True)
            z_bf = tile([P, PIECE, PACK], BF16, "z%d" % c)
            nc.scalar.activation(z_bf[:], u[:].rearrange("p t n -> p n t"), SILU)
            return z_bf

        def second_layer(c, z_bf):
            z_codes = tile([P, PIECE], U32, "z_codes%d" % c)
            z_scales = tile([P, PIECE], U8, "z_scales%d" % c)
            nc.vector.quantize_mx(z_codes[:].bitcast(FP8X4), z_scales[:], z_bf[:].rearrange("p n t -> p (n t)"))
            acc = ps.tile([P, PACK, PIECE], F32, name="acc%d" % c, tag="bank%d" % (PACK + c))
            for t in range(PACK):
                cols = slice(t * P, (t + 1) * P)
                nc.tensor.matmul_mx(
                    acc[:, t, :],
                    lhsT=w2_codes[:, cols].bitcast(FP8X4),
                    lhsT_scale=w2_sc[:, cols],
                    rhs=z_codes[:].bitcast(FP8X4),
                    rhs_scale=z_scales[:],
                    start=True,
                    stop=True,
                )
            return acc

        def store(c, acc, o_bf):
            o_f32 = tile([P, PACK, PIECE], F32, "o_f32%d" % c)
            if c == 3:
                nc.vector.tensor_copy(o_bf, acc[:].rearrange("p t n -> p n t"))
            (nc.vector.tensor_copy if c == 0 else nc.scalar.copy)(o_f32[:], acc[:])
            nc.sync.dma_start(out_rows[:, :, c * PIECE : (c + 1) * PIECE], o_f32[:])
            if c < 3:
                nc.vector.tensor_copy(woven(o_bf), planar(o_f32[:]))

        def hand_on(half, o_bf):
            o_codes = tile([P, HALF], I32, "o_codes%d" % half)
            cols = slice(half * HALF, (half + 1) * HALF)
            nc.vector.quantize_mx(o_codes[:].bitcast(FP8X4), o_scales[:, cols], o_bf[:].rearrange("p n t -> p (n t)"))
            nc.sync.dma_start(out_words[:, cols], o_codes[:])

        z = [hidden(c) for c in range(PIECES)]
        accs = [second_layer(c, z[c]) for c in range(PIECES)]
        for half in range(2):
            o_bf = tile([P, HALF, PACK], BF16, "o_bf%d" % half)
            for c in range(2):
                store(2 * half + c, accs[2 * half + c], o_bf[:, c * PIECE : (c + 1) * PIECE, :])
            hand_on(half, o_bf)
        for q in range(QUADS):
            queue = nc.sync if q % 2 else nc.scalar
            queue.dma_start(
                out_2[0, 4 * q : 4 * q + 4, :].bitcast(I32), o_scales[32 * q : 32 * q + 4, :].bitcast(I32)
            )
